import numpy as np, ml_dtypes
CORES = [2,3,42,43,82,83,122,123]
N = 8
import mx_ref
BF = ml_dtypes.bfloat16
def entries(a):
    return np.ascontiguousarray(a.T).reshape(-1)
def table(e):
    return np.ascontiguousarray(np.reshape(e, (-1, 16)).T).astype(np.int32)
def pick(q, e):
    c = np.concatenate([q[0].reshape(128, -1, 4), np.zeros((128, 1, 4), np.uint8)], axis=1); s = np.concatenate([q[1], np.ones((16, 1), np.uint8)], axis=1)
    return (np.ascontiguousarray(c[:, e].reshape(128, -1)), np.ascontiguousarray(s[:, e]))
def join(*qs):
    return (np.concatenate([q[0] for q in qs], axis=1), np.concatenate([q[1] for q in qs], axis=1))
def put(q, e, v):
    c, s = q[0].reshape(128, -1, 4).copy(), q[1].copy(); c[:, e] = v[0].reshape(128, -1, 4); s[:, e] = v[1]
    return (c.reshape(128, -1), s)
def pk(c, s):
    return (np.ascontiguousarray(c), mx_ref.live(s))
def emit(q):
    return q[0], q[1]
def packed(v, rng):
    q = [mx_ref.quantize(np.ascontiguousarray(v[r])) for r in range(N)]
    return np.stack([a for a, b in q]), np.stack([mx_ref.plane(b, rng) for a, b in q])
def cols(t, e):
    v = np.concatenate([t.reshape(128, -1, 4), np.zeros((128, 1, 4), BF)], axis=1)
    return np.ascontiguousarray(v[:, e]).reshape(128, -1)
def f(rng, *shape):
    return mx_ref.flush((rng.standard_normal(shape, dtype=np.float32) * np.exp2(rng.integers(-2, 3, shape[:-1] + (1,)))).astype(BF))
def wide(rng, *shape, cols=0):
    v = rng.standard_normal(shape, dtype=np.float32) * np.exp2(rng.integers(-12, 13, shape)).astype(np.float32)
    if cols: v *= np.repeat(np.exp2(rng.integers(-cols, cols + 1, shape[:-2] + (1, shape[-1] // 4))) * (rng.random(shape[:-2] + (1, shape[-1] // 4)) > 0.0625), 4, axis=-1).astype(np.float32)
    return mx_ref.flush(v.astype(BF))
T, C, CAPP, M = 256, 512, 32, 128
def first(v):
    z = np.zeros((N, 128, 512), BF); z[:, :, :4] = v; return z
def lists(rng, full=False, one=False, odd=False):
    h = int(rng.integers(0, N)); a = rng.permutation(np.delete(np.arange(N), h))
    sn = np.full((N, N, CAPP), -1)
    for d in range(N):
        m, o = int(rng.integers(1, M + 1)), rng.permutation(N * CAPP)
        if odd: m = 2 * int(rng.integers(0, M // 2)) + 1
        if full:
            w = np.isin(o // CAPP, a[:M // CAPP] if d == h else a[:1]); o = np.concatenate([o[w], o[~w]])
            m = M if d == h else int(rng.integers(CAPP, M + 1))
        if one: o = o[o // CAPP != a[0]]
        if one and d == h: m, o = 1, o[o // CAPP != h]
        o = o[:m]
        sn[o // CAPP, d, o % CAPP] = rng.integers(0, T, m)
    return np.stack([table(sn[s]) for s in range(N)])
def setup_inputs(rng):
    kc, ks = packed(f(rng, N, 128, 4 * C), rng)
    return {"x": f(rng, N, 128, 4 * T), "u": first(f(rng, N, 128, 4)), "w": f(rng, N, 128, 512), "kc": kc, "ks": ks, "sn": lists(rng)}
def setup_inputs_full(rng):
    return {**setup_inputs(rng), "sn": lists(rng, full=True)}
def setup_inputs_high(rng):
    d = setup_inputs(rng); g = np.where(rng.permutation(N) < N // 2, 1, -1).astype(np.float32)[:, None, None]
    p = rng.permutation(N)
    g = g * np.where(p < N // 2, 2.0 ** 24, 2.0 ** -24).astype(np.float32)[:, None, None]
    k = np.where(p == N - 1, 2.0 ** -24, 2.0 ** 24).astype(np.float32)[:, None, None]
    d["u"] = first(((np.abs(f(rng, N, 128, 4).astype(np.float32)) + 1) * k).astype(BF))
    d["kc"], d["ks"] = packed((g * (1 + np.abs(f(rng, N, 128, 4 * C).astype(np.float32)))).astype(BF), rng); return d
def setup_inputs_one(rng):
    return {**setup_inputs(rng), "sn": lists(rng, one=True)}
def setup_inputs_spread(rng):
    d = setup_inputs(rng); d["x"] = wide(rng, N, 128, 4 * T, cols=8)
    d["kc"], d["ks"] = packed(wide(rng, N, 128, 4 * C, cols=8), rng); return d
def setup_inputs_ties(rng):
    d = setup_inputs(rng); v = f(rng, N, 128, C // 8 * 4)
    d["kc"], d["ks"] = packed(np.stack([cols(v[r], rng.permutation(np.arange(C) // 8)) for r in range(N)]), rng)
    d["u"][int(rng.integers(0, N))] = 0
    d["sn"] = lists(rng, odd=True); return d
def scores(u, kc, ks):
    return mx_ref.matmul(mx_ref.quantize(np.ascontiguousarray(u)), pk(kc, ks))[0] + np.float32(0)
def check_inputs(d):
    b = []
    for r in range(N):
        if (d["u"][r][:, 4:].astype(np.float32) != 0).any(): b.append("u")
        e = entries(d["sn"][r])
        m = sum(int((entries(d["sn"][s])[r * CAPP:r * CAPP + CAPP] >= 0).sum()) for s in range(N))
        if e.min() < -1 or e.max() >= T or m < 1 or m > M: b.append("sn")
        try: good = bool(np.isfinite(scores(d["u"][r], d["kc"][r], d["ks"][r])).all())
        except Exception: good = False
        if not good: b.append("kc")
    return b
def reference(x, u, w, kc, ks, sn):
    oc, osc, ev = np.zeros((N, 128, 4 * C), np.uint8), np.zeros((N, 16, C), np.uint8), np.zeros((N, 2, M), np.float32)
    y = np.zeros((N, 128, C), np.float32)
    new = join(*[mx_ref.quantize(np.ascontiguousarray(x[s])) for s in range(N)])
    for d in range(N):
        e = []
        for s in range(N):
            v = entries(sn[s])[d * CAPP:d * CAPP + CAPP]; e.append(s * T + v[v >= 0])
        e = np.concatenate(e); m = e.size
        z = scores(u[d], kc[d], ks[d])
        out = np.argsort(z, kind="stable")[:m]
        after = put(pk(kc[d], ks[d]), out, pick(new, e))
        oc[d], osc[d] = emit(after)
        ev[d, 0] = -1; ev[d, 0, :m] = out; ev[d, 1, :m] = z[out]
        y[d] = mx_ref.matmul(mx_ref.quantize(np.ascontiguousarray(w[d])), after)
    return {"oc": oc, "osc": osc, "ev": ev, "y": y}

@@ -1,0 +1,325 @@
+from concourse.bass import DstId, RemoteDMATransfer
+from concourse.mybir import dt, AluOpType as A, AxisListType, ActivationFunctionType as F
+
+N, CAPP, TX, C, M = 8, 32, 256, 512, 128
+X4, U8, F32, BF, I32, U16 = "float8_e4m3fn_x4", "uint8", "float32", "bfloat16", "int32", "uint16"
+
+
+def _sb(n, d):
+    return ("sbuf", [128, n], d)
+
+
+SCRATCH = {
+    "snr": _sb(16, I32), "snoff": _sb(16, U16), "va": _sb(8, F32), "vb": _sb(8, F32), "vf": _sb(8, F32),
+    "xt": _sb(1024, BF), "xq": _sb(256, X4), "xs": _sb(256, U8),
+    "slq": _sb(256, X4), "sls": _sb(256, U8), "slots": _sb(256, X4), "slotss": _sb(256, U8),
+    "cand": _sb(640, X4), "cands": _sb(640, U8), "aft": _sb(512, X4), "afts": _sb(512, U8),
+    "uw": _sb(4, BF), "ut": _sb(512, BF), "uq": _sb(128, X4), "us": _sb(128, U8),
+    "wt": _sb(512, BF), "wq": _sb(128, X4), "ws": _sb(128, U8),
+    "p4i": _sb(32, I32), "p4j": _sb(32, I32), "off4": _sb(32, U16),
+    "pidx": _sb(2, I32), "hbit": _sb(2, I32), "qi": _sb(2, I32), "hm": _sb(1, F32), "hn": _sb(1, F32), "qf": _sb(1, F32),
+    "jw": _sb(32, I32), "j128": _sb(32, I32), "k16": _sb(8, F32), "k16q": _sb(8, F32), "thr": _sb(8, F32),
+    "mu": _sb(512, F32), "ones": _sb(32, F32), "zer": _sb(256, F32),
+    "lv": _sb(8, F32), "bc": _sb(256, F32), "vrow": _sb(256, F32), "pre": _sb(256, F32),
+    "acc": _sb(8, F32), "sel": _sb(8, F32), "soff": _sb(8, U16), "junk": _sb(2048, BF), "junk2": _sb(2048, BF),
+    "ns": _sb(4, F32), "dd": _sb(512, F32), "cm": _sb(2048, BF), "rk": _sb(4, F32), "rex": _sb(4, F32), "rr": _sb(4, F32),
+    "rh": _sb(2, F32), "tb": _sb(64, F32), "tbt": _sb(64, F32), "rb": _sb(288, F32), "tt1": _sb(256, F32), "tt2": _sb(288, F32),
+    "pwa": _sb(16, F32), "pwb": _sb(16, F32), "pw": _sb(16, I32), "rw": _sb(32, I32), "fm": _sb(32, I32), "foff": _sb(32, U16),
+    "evin": _sb(512, F32), "evw": _sb(640, F32), "ysb": _sb(512, F32),
+    "prow": ("psum", [128, 512], F32), "prow2": ("psum", [128, 512], F32),
+    "pc0": ("psum", [128, 512], F32), "pc1": ("psum", [128, 512], F32), "pc2": ("psum", [128, 512], F32), "pc3": ("psum", [128, 512], F32),
+    "py": ("psum", [128, 1024], F32),
+}
+SEMAPHORES = ["v", "s", "t", "gq", "d_sn", "d_x", "d_u", "d_k", "d_w", "d_ev", "d_out", "larr", "arrc", "arrs", "loc"]
+
+
+def _plan(T, topo, s):
+    me = T.cores[s]
+    rest = [(s + k) % N for k in range(1, N)]
+    on = [d for d in rest if topo.chip(T.cores[d]) == topo.chip(me)]
+    off = [d for d in rest if topo.chip(T.cores[d]) != topo.chip(me)]
+    e_off = topo.engines(me, T.cores[off[0]])
+    e_on = [e for e in topo.engines(me, T.cores[on[0]]) if e not in e_off]
+    return on, off, e_off, e_on[:len(e_on) // 2]
+
+
+def _list_engines(T, topo, s):
+    on, off, e_off, e_on = _plan(T, topo, s)
+    r, k = {on[0]: e_on}, 0
+    spare = len(e_off) - len(off)
+    for i, d in enumerate(off):
+        n = 2 if i < spare else 1
+        r[d] = e_off[k:k + n]
+        k += n
+    return r
+
+
+def _data_engines(T, topo, s):
+    on, off, e_off, e_on = _plan(T, topo, s)
+    q, h = len(e_off) // 4, len(e_off) // 2
+    a = {d: e_off[q * i:q * i + q] for i, d in enumerate(off[:4])}
+    a[on[0]] = e_on
+    b = {d: e_off[h * i:h * i + h] for i, d in enumerate(off[4:])}
+    return a, b
+
+
+def rank_program(g, core, T, topo):
+    r = T.rank_of(core)
+    if r is None:
+        return
+    sem = T.sem
+    cnt = {"v": 0, "s": 0, "t": 0, "gq": 0}
+    seen = {}
+    qs = {"v": g.vector, "s": g.scalar, "t": g.tensor, "gq": g, "y": g.sync}
+
+    def need(q, *deps):
+        for name, val in deps:
+            if seen.get((q, name), 0) < val:
+                qs[q].wait_ge(sem[name], val)
+                seen[(q, name)] = val
+
+    def done(q, ins):
+        ins.then_inc(sem[q], 1)
+        cnt[q] += 1
+        return (q, cnt[q])
+
+    V, S, Y = g.vector, g.scalar, g.sync
+    dma = {}
+
+    def load(q, name, out, in_):
+        q.dma_start(out, in_).then_inc(sem[name], 16)
+        dma[name] = dma.get(name, 0) + 16
+
+    load(Y, "d_x", T.xt[:], T.x[:])
+    for k in range(8):
+        load(S, "d_sn", T.snr[16 * k:16 * k + 16, :], T.sn[:])
+    load(S, "d_u", T.uw[:], T.u[:, 0:4])
+    load(Y, "d_k", T.cand[:, M:M + C].bitcast(dt.uint8), T.kc[:])
+    load(Y, "d_k", T.cands[:, M:M + C], T.ks[:])
+    load(Y, "d_w", T.wt[:], T.w[:])
+
+    g_p4 = done("gq", g.iota(T.p4i[:], [[0, 32]], 0, 1))
+    g_pi = done("gq", g.iota(T.pidx[:], [[0, 2]], 0, 1))
+    g_jw = done("gq", g.iota(T.jw[:], [[16, 32]], M, 0))
+    g_k16 = done("gq", g.iota(T.k16[:], [[16, 8]], 0, 0, allow_small_or_imprecise_dtypes=True))
+    v_mu = done("v", V.memset(T.mu[:], 1e-35))
+    need("v", g_p4)
+    a = done("v", V.tensor_scalar(T.p4j[:], T.p4i[:], 3, None, A.bitwise_and))
+    need("v", g_pi)
+    b = done("v", V.tensor_scalar(T.hbit[:], T.pidx[:], 4, 1, A.arith_shift_right, A.bitwise_and))
+    c = done("v", V.tensor_scalar(T.qi[:], T.pidx[:], 15, None, A.bitwise_and))
+    need("v", a)
+    v_off4 = done("v", V.tensor_copy(T.off4[:], T.p4j[:]))
+    need("v", b)
+    v_hm = done("v", V.tensor_copy(T.hm[:], T.hbit[:, 0:1]))
+    need("v", c)
+    v_qf = done("v", V.tensor_copy(T.qf[:], T.qi[:, 0:1]))
+    need("v", v_hm)
+    v_hn = done("v", V.tensor_scalar(T.hn[:], T.hm[:], -1.0, 1.0, A.mult, A.add))
+    need("v", v_qf, g_jw, g_k16)
+    v_j128 = done("v", V.tensor_scalar(T.j128[:], T.jw[:], T.qf[:], None, A.add))
+    a = done("v", V.tensor_scalar(T.k16q[:], T.k16[:], T.qf[:], None, A.add))
+    v_one = done("v", V.memset(T.ones[:], 1.0))
+    need("v", a)
+    v_thr = done("v", V.tensor_scalar(T.thr[:], T.k16q[:], -1.0, -0.5, A.mult, A.add))
+    v_zer = done("v", V.memset(T.zer[:], 0.0))
+    v_tb = done("v", V.memset(T.tb[:], 0.0))
+    v_rb = done("v", V.memset(T.rb[:], 0.0))
+    a = done("v", V.memset(T.evw[:, 0:M], 0.0))
+    need("v", a)
+    v_evw = done("v", V.memset(T.evw[0:32, 0:M], -1.0))
+    need("gq", v_mu)
+    g_mu = done("gq", g.affine_select(T.mu[:], T.mu[:], [[0, 4], [-1, 128]], A.is_gt, 0.0, 0, 1))
+    g_ev = done("gq", g.iota(T.evin[:], [[1, C]], 0, 0, allow_small_or_imprecise_dtypes=True))
+
+    need("v", ("d_sn", dma["d_sn"]), v_hn)
+    a = done("v", V.tensor_scalar(T.va[:], T.snr[:, 0:16:2], 0.0, T.hn[:], A.is_ge, A.mult))
+    b = done("v", V.tensor_scalar(T.vb[:], T.snr[:, 1:16:2], 0.0, T.hm[:], A.is_ge, A.mult))
+    v_sno = done("v", V.tensor_copy(T.snoff[:], T.snr[:]))
+    need("v", a, b)
+    v_vf = done("v", V.tensor_tensor(T.vf[:], T.va[:], T.vb[:], A.add))
+
+    need("s", v_off4, ("d_u", dma["d_u"]))
+    s_ut = done("s", S.activation(T.ut[:], T.uw[:].indirect(T.off4[:]), F.Copy))
+    need("v", s_ut)
+    v_uq = done("v", V.quantize_mx(T.uq[:], T.us[:], T.ut[:]))
+
+    need("v", ("d_x", dma["d_x"]))
+    v_xq = done("v", V.quantize_mx(T.xq[:], T.xs[:], T.xt[:]))
+    need("v", v_xq, v_sno)
+    v_sl = done("v", V.tensor_copy(T.slq[:].bitcast(dt.uint32), T.xq[:].bitcast(dt.uint32).indirect(T.snoff[:, 0:16])))
+    o = CAPP * r
+    v_own = done("v", V.tensor_copy(T.slots[:, o:o + CAPP].bitcast(dt.uint32),
+                                    T.xq[:].bitcast(dt.uint32).indirect(T.snoff[:, 2 * r:2 * r + 2])))
+    need("s", v_xq, v_sno)
+    s_sl = done("s", S.activation(T.sls[:], T.xs[:].indirect(T.snoff[:, 0:16]), F.Copy))
+    s_own = done("s", S.activation(T.slotss[:, o:o + CAPP], T.xs[:].indirect(T.snoff[:, 2 * r:2 * r + 2]), F.Copy))
+
+    local = [0]
+
+    def send(engs, src, dst, rs):
+        tr = []
+        for d, es in engs.items():
+            rid, pid, _ = topo.addr(T.cores[d])
+            m = 0
+            for e in es:
+                m |= 1 << e
+            tr.append(RemoteDMATransfer(dst_ids=[DstId(rid=rid, pnc=pid)], dma_engine_mask=m, remote_sem=sem[rs],
+                                        srcs=[src(d)], dsts=[dst]))
+            local[0] += len(es)
+        g.remote_dma_fused(tr, local_sem=sem["loc"])
+
+    need("gq", v_vf)
+    send(_list_engines(T, topo, r), lambda d: T.vf[:, d:d + 1], T.lv[:, r:r + 1], "larr")
+    ea, eb = _data_engines(T, topo, r)
+    csrc = lambda d: T.slq[:, CAPP * d:CAPP * d + CAPP].bitcast(dt.uint8)
+    ssrc = lambda d: T.sls[:, CAPP * d:CAPP * d + CAPP]
+    cdst, sdst = T.slots[:, o:o + CAPP].bitcast(dt.uint8), T.slotss[:, o:o + CAPP]
+    need("gq", v_sl)
+    send(ea, csrc, cdst, "arrc")
+    send(eb, csrc, cdst, "arrc")
+    need("gq", s_sl)
+    send(ea, ssrc, sdst, "arrs")
+    send(eb, ssrc, sdst, "arrs")
+
+    need("t", v_uq, ("d_k", dma["d_k"]))
+    t_pc = [done("t", g.tensor.matmul_mx(T["pc%d" % k][:, 0:128], T.cand[:, M + 128 * k:M + 128 * k + 128],
+                                         T.cands[:, M + 128 * k:M + 128 * k + 128], T.uq[:], T.us[:], True, True)) for k in range(4)]
+    t_row = done("t", g.tensor.matmul_mx(T.prow[:], T.uq[:], T.us[:], T.cand[:, M:M + C], T.cands[:, M:M + C], True, True))
+    t_row2 = done("t", g.tensor.matmul_mx(T.prow2[:], T.uq[:], T.us[:], T.cand[:, M:M + C], T.cands[:, M:M + C], True, True))
+    need("v", ("d_w", dma["d_w"]))
+    v_wq = done("v", V.quantize_mx(T.wq[:], T.ws[:], T.wt[:]))
+    for k in range(4):
+        need("v", t_pc[k])
+        v_ns = done("v", V.tensor_scalar(T.ns[:, k:k + 1], T["pc%d" % k][:, 0:1], -1.0, None, A.mult))
+
+    need("s", v_ns, t_row2)
+    s_d = [done("s", S.activation(T.dd[:, 128 * k:128 * k + 128], T.prow2[:, 128 * k:128 * k + 128], F.Identity,
+                                  bias=T.ns[:, k:k + 1])) for k in range(4)]
+    need("v", t_row, v_ns)
+    v_cm = {}
+
+    def outer(k):
+        lo, hi = 128 * k, 128 * k + 128
+        if k > 0:
+            done("v", V.tensor_scalar(T.cm[:, 512 * k:512 * k + lo], T.prow[:, 0:lo], T.ns[:, k:k + 1], 0.0, A.add, A.is_le))
+        if k < 3:
+            done("v", V.tensor_scalar(T.cm[:, 512 * k + hi:512 * k + 512], T.prow[:, hi:512], T.ns[:, k:k + 1], 0.0, A.add, A.is_lt))
+
+    def inner(k):
+        need("v", s_d[k], g_mu)
+        v_cm[k] = done("v", V.tensor_tensor(T.cm[:, 640 * k:640 * k + 128], T.dd[:, 128 * k:128 * k + 128],
+                                            T.mu[:, 128 * k:128 * k + 128], A.is_lt))
+
+    outer(0)
+    outer(1)
+    inner(0)
+    outer(2)
+    inner(1)
+    outer(3)
+    inner(2)
+    inner(3)
+    for k in range(3):
+        need("s", v_cm[k])
+        s_rk = done("s", S.activation(T.junk[:, 512 * k:512 * k + 512], T.cm[:, 512 * k:512 * k + 512], F.Copy, accum_out=T.rk[:, k:k + 1]))
+    lneed = 0
+    for s in range(N):
+        if s != r:
+            lneed += len(_list_engines(T, topo, s)[r])
+    need("v", ("larr", lneed), v_one)
+    for s in range(N):
+        col = T.vf[:, r:r + 1] if s == r else T.lv[:, s:s + 1]
+        a = done("v", V.tensor_scalar(T.bc[:, 32 * s:32 * s + 32], T.ones[:], col, None, A.mult))
+    need("v", a)
+    a = done("v", V.transpose(T.vrow[:], T.bc[:]))
+    need("v", a, v_zer)
+    v_pre = done("v", V.tensor_tensor_scan(T.pre[:], T.vrow[:], T.zer[:], 0.0, A.add, A.add))
+    need("v", v_cm[3])
+    v_rk = done("v", V.tensor_reduce(T.rk[:, 3:4], T.cm[:, 1536:2048], AxisListType.X, A.add))
+
+    need("v", s_rk, v_rk, v_pre)
+    a = done("v", V.tensor_scalar(T.rex[:], T.rk[:], T.pre[:, 255:256], 2048.0, A.is_ge, A.mult))
+    need("v", a)
+    a = done("v", V.tensor_tensor(T.rr[:], T.rk[:], T.rex[:], A.add))
+    need("v", a)
+    a = done("v", V.tensor_scalar(T.rh[:], T.rr[:, 2:4], 4096.0, None, A.mult))
+    need("v", a, v_tb)
+    a = done("v", V.tensor_tensor(T.tb[:, 0:64:32], T.rh[:], T.rr[:, 0:2], A.add))
+    need("v", a)
+    v_tbt = done("v", V.transpose(T.tbt[:], T.tb[:]))
+    need("gq", v_tbt, v_rb)
+    for k in range(4):
+        g_rb = done("gq", g.partition_broadcast(T.rb[:, 16 + 64 * k:80 + 64 * k], T.tbt[32 * k:32 * k + 1, :], 128))
+    need("v", g_rb)
+    a = done("v", V.transpose(T.tt1[:], T.rb[:, 16:272]))
+    b = done("v", V.transpose(T.tt2[:], T.rb[:]))
+    need("v", a, b)
+    for k in range(2):
+        t1, ta, tb = T.tt1[:, 32 * k:256:64], T.tt2[:, 32 * k:256:64], T.tt2[:, 32 * k + 32:288:64]
+        done("v", V.tensor_scalar(T.pwa[:, 8 * k:8 * k + 8:2], t1, T.hn[:], None, A.mult))
+        done("v", V.tensor_scalar(T.pwb[:, 8 * k:8 * k + 8:2], ta, T.hm[:], None, A.mult))
+        done("v", V.tensor_scalar(T.pwa[:, 8 * k + 1:8 * k + 8:2], tb, T.hn[:], None, A.mult))
+        a = done("v", V.tensor_scalar(T.pwb[:, 8 * k + 1:8 * k + 8:2], t1, T.hm[:], None, A.mult))
+    need("v", a)
+    a = done("v", V.tensor_tensor(T.pw[:], T.pwa[:], T.pwb[:], A.add))
+    need("v", a)
+    done("v", V.tensor_scalar(T.rw[:, 0:16], T.pw[:], 4095, None, A.bitwise_and))
+    a = done("v", V.tensor_scalar(T.rw[:, 16:32], T.pw[:], 12, None, A.arith_shift_right))
+    need("v", a, v_j128)
+    a = done("v", V.tensor_tensor(T.fm[:], T.rw[:], T.j128[:], A.min))
+    need("v", a)
+    v_fo = done("v", V.tensor_copy(T.foff[:], T.fm[:]))
+
+    need("s", g_ev)
+    s_ev = done("s", S.activation(T.evin[32:64, :], T.prow2[32:64, :], F.Copy))
+    need("s", v_pre, v_thr)
+    for k in range(8):
+        s_acc = done("s", S.activation(T.junk2[:, 256 * k:256 * k + 256], T.pre[:], F.Sign, bias=T.thr[:, k:k + 1], accum_out=T.acc[:, k:k + 1]))
+    need("v", s_acc)
+    a = done("v", V.tensor_scalar(T.sel[:], T.acc[:], -0.5, 128.0, A.mult, A.add))
+    need("v", a)
+    v_so = done("v", V.tensor_scalar(T.soff[:], T.sel[:], 255.0, None, A.min))
+
+    need("v", s_ev, v_fo, v_evw)
+    v_ev = done("v", V.tensor_copy(T.evw[:].indirect(T.foff[:]), T.evin[:]))
+    need("y", v_ev)
+    load(Y, "d_ev", T.ev[0:1, :], T.evw[0:1, 0:M])
+    load(Y, "d_ev", T.ev[1:2, :], T.evw[32:33, 0:M])
+
+    aneed = 0
+    for s in range(N):
+        if s != r:
+            x, y = _data_engines(T, topo, s)
+            aneed += len({**x, **y}[r])
+    need("v", v_so, ("arrc", aneed), v_own)
+    v_ar = done("v", V.tensor_copy(T.cand[:, 0:M].bitcast(dt.uint32), T.slots[:].bitcast(dt.uint32).indirect(T.soff[:])))
+    need("s", v_so, ("arrs", aneed), s_own)
+    s_ar = done("s", S.activation(T.cands[:, 0:M], T.slotss[:].indirect(T.soff[:]), F.Copy))
+    need("v", v_ar, ("d_k", dma["d_k"]))
+    need("s", s_ar, v_fo, ("d_k", dma["d_k"]))
+    v_af, s_af, t_y = [], [], []
+    for k in range(2):
+        f = T.foff[:, 16 * k:16 * k + 16]
+        v_af.append(done("v", V.tensor_copy(T.aft[:, 256 * k:256 * k + 256].bitcast(dt.uint32), T.cand[:].bitcast(dt.uint32).indirect(f))))
+        s_af.append(done("s", S.activation(T.afts[:, 256 * k:256 * k + 256], T.cands[:].indirect(f), F.Copy)))
+        need("t", v_af[k], s_af[k], v_wq)
+        t_y.append(done("t", g.tensor.matmul_mx(T.py[:, 512 * k:512 * k + 256], T.wq[:], T.ws[:], T.aft[:, 256 * k:256 * k + 256],
+                                                T.afts[:, 256 * k:256 * k + 256], True, True)))
+        need("y", v_af[k])
+        load(Y, "d_out", T.oc[:, 1024 * k:1024 * k + 1024], T.aft[:, 256 * k:256 * k + 256].bitcast(dt.uint8))
+    need("s", t_y[0])
+    s_y = done("s", S.activation(T.ysb[:, 0:256], T.py[:, 0:256], F.Copy))
+    need("v", t_y[1])
+    v_y = done("v", V.tensor_copy(T.ysb[:, 256:512], T.py[:, 512:768]))
+    need("s", s_y)
+    load(S, "d_out", T.y[:, 0:256], T.ysb[:, 0:256])
+    need("y", s_af[1])
+    for k in range(4):
+        load(Y, "d_out", T.osc[4 * k:4 * k + 4, :], T.afts[32 * k:32 * k + 4, :])
+    need("y", v_y)
+    load(Y, "d_out", T.y[:, 256:512], T.ysb[:, 256:512])
+
+    for n, val in cnt.items():
+        need("y", (n, val))
+    need("y", ("d_ev", dma["d_ev"]), ("d_out", dma["d_out"]))
+    need("gq", ("loc", local[0]))

@@ -1,7 +1,7 @@
 from concourse.bass import DstId, RemoteDMATransfer
-from concourse.mybir import dt, AluOpType as A, AxisListType, ActivationFunctionType as F
+from concourse.mybir import dt, AluOpType as A, ActivationFunctionType as F
 
-N, CAPP, TX, C, M = 8, 32, 256, 512, 128
+N, CAPP, C, M = 8, 32, 512, 128
 X4, U8, F32, BF, I32, U16 = "float8_e4m3fn_x4", "uint8", "float32", "bfloat16", "int32", "uint16"
 
 
@@ -19,47 +19,42 @@ SCRATCH = {
     "p4i": _sb(32, I32), "p4j": _sb(32, I32), "off4": _sb(32, U16),
     "pidx": _sb(2, I32), "hbit": _sb(2, I32), "qi": _sb(2, I32), "hm": _sb(1, F32), "hn": _sb(1, F32), "qf": _sb(1, F32),
     "jw": _sb(32, I32), "j128": _sb(32, I32), "k16": _sb(8, F32), "k16q": _sb(8, F32), "thr": _sb(8, F32),
-    "mu": _sb(512, F32), "ones": _sb(32, F32), "zer": _sb(256, F32),
+    "mu": _sb(128, F32), "ones": _sb(32, F32),
     "lv": _sb(8, F32), "bc": _sb(256, F32), "vrow": _sb(256, F32), "pre": _sb(256, F32),
-    "acc": _sb(8, F32), "sel": _sb(8, F32), "soff": _sb(8, U16), "junk": _sb(2048, BF), "junk2": _sb(2048, BF),
-    "ns": _sb(4, F32), "dd": _sb(512, F32), "cm": _sb(2048, BF), "rk": _sb(4, F32), "rex": _sb(4, F32), "rr": _sb(4, F32),
-    "rh": _sb(2, F32), "tb": _sb(64, F32), "tbt": _sb(64, F32), "rb": _sb(288, F32), "tt1": _sb(256, F32), "tt2": _sb(288, F32),
-    "pwa": _sb(16, F32), "pwb": _sb(16, F32), "pw": _sb(16, I32), "rw": _sb(32, I32), "fm": _sb(32, I32), "foff": _sb(32, U16),
+    "acc": _sb(8, F32), "soff": _sb(8, U16), "junk": _sb(2048, BF), "junk2": _sb(2048, BF),
+    "ns": _sb(4, F32), "dd": _sb(512, F32), "cm": _sb(2048, BF), "rk": _sb(4, F32),
+    "tb0": _sb(32, F32), "tb1": _sb(32, F32), "tbt0": _sb(32, F32), "tbt1": _sb(32, F32), "rb0": _sb(160, F32), "rb1": _sb(160, F32),
+    "ta0": _sb(128, F32), "ta1": _sb(128, F32), "tc0": _sb(160, F32), "tc1": _sb(160, F32),
+    "pwa0": _sb(8, F32), "pwa1": _sb(8, F32), "pwb0": _sb(8, F32), "pwb1": _sb(8, F32), "pw0": _sb(8, I32), "pw1": _sb(8, I32),
+    "rw": _sb(32, I32), "ge": _sb(32, I32), "rm": _sb(32, I32), "fm": _sb(32, I32), "foff": _sb(32, U16),
     "evin": _sb(512, F32), "evw": _sb(640, F32), "ysb": _sb(512, F32),
-    "prow": ("psum", [128, 512], F32), "prow2": ("psum", [128, 512], F32),
+    "ra": ("psum", [128, 512], F32), "rc": ("psum", [128, 512], F32), "sa": ("psum", [128, 512], F32), "sc": ("psum", [128, 512], F32),
     "pc0": ("psum", [128, 512], F32), "pc1": ("psum", [128, 512], F32), "pc2": ("psum", [128, 512], F32), "pc3": ("psum", [128, 512], F32),
-    "py": ("psum", [128, 1024], F32),
 }
-SEMAPHORES = ["v", "s", "t", "gq", "d_sn", "d_x", "d_u", "d_k", "d_w", "d_ev", "d_out", "larr", "arrc", "arrs", "loc"]
+SEMAPHORES = ["v", "s", "t", "gq", "d_sn", "d_x", "d_u", "d_k0", "d_k1", "d_w", "d_ev", "d_out", "larr", "arrc", "arrs", "loc"]
 
 
-def _plan(T, topo, s):
+def _deal(dst, engs):
+    r, k = {}, 0
+    two = len(engs) - len(dst)
+    for n, d in enumerate(dst):
+        w = 2 if n >= len(dst) - two else 1
+        r[d] = engs[k:k + w]
+        k += w
+    return r
+
+
+def _engines(T, topo, s):
     me = T.cores[s]
     rest = [(s + k) % N for k in range(1, N)]
     on = [d for d in rest if topo.chip(T.cores[d]) == topo.chip(me)]
     off = [d for d in rest if topo.chip(T.cores[d]) != topo.chip(me)]
     e_off = topo.engines(me, T.cores[off[0]])
     e_on = [e for e in topo.engines(me, T.cores[on[0]]) if e not in e_off]
-    return on, off, e_off, e_on[:len(e_on) // 2]
-
-
-def _list_engines(T, topo, s):
-    on, off, e_off, e_on = _plan(T, topo, s)
-    r, k = {on[0]: e_on}, 0
-    spare = len(e_off) - len(off)
-    for i, d in enumerate(off):
-        n = 2 if i < spare else 1
-        r[d] = e_off[k:k + n]
-        k += n
-    return r
-
-
-def _data_engines(T, topo, s):
-    on, off, e_off, e_on = _plan(T, topo, s)
-    q, h = len(e_off) // 4, len(e_off) // 2
-    a = {d: e_off[q * i:q * i + q] for i, d in enumerate(off[:4])}
-    a[on[0]] = e_on
-    b = {d: e_off[h * i:h * i + h] for i, d in enumerate(off[4:])}
+    h = len(e_off) // 2
+    a = _deal(off, e_off)
+    b = _deal(off[2:] + off[:2], e_off[h:] + e_off[:h])
+    a[on[0]] = b[on[0]] = e_on[:len(e_on) // 4]
     return a, b
 
 
@@ -89,20 +84,24 @@ def rank_program(g, core, T, topo):
     def load(q, name, out, in_):
         q.dma_start(out, in_).then_inc(sem[name], 16)
         dma[name] = dma.get(name, 0) + 16
+        return (name, dma[name])
 
-    load(Y, "d_x", T.xt[:], T.x[:])
-    for k in range(8):
-        load(S, "d_sn", T.snr[16 * k:16 * k + 16, :], T.sn[:])
-    load(S, "d_u", T.uw[:], T.u[:, 0:4])
-    load(Y, "d_k", T.cand[:, M:M + C].bitcast(dt.uint8), T.kc[:])
-    load(Y, "d_k", T.cands[:, M:M + C], T.ks[:])
-    load(Y, "d_w", T.wt[:], T.w[:])
+    for k in range(4):
+        load(Y, "d_sn", T.snr[16 * k:16 * k + 16, :], T.sn[:])
+        d_sn = load(S, "d_sn", T.snr[64 + 16 * k:80 + 16 * k, :], T.sn[:])
+    d_u = load(S, "d_u", T.uw[:], T.u[:, 0:4])
+    d_x = load(Y, "d_x", T.xt[:], T.x[:])
+    d_k = []
+    for k in range(2):
+        a, b = 256 * k, 256 * k + 256
+        load(Y, "d_k%d" % k, T.cand[:, M + a:M + b].bitcast(dt.uint8), T.kc[:, 4 * a:4 * b])
+        d_k.append(load(Y, "d_k%d" % k, T.cands[:, M + a:M + b], T.ks[:, a:b]))
+    d_w = load(Y, "d_w", T.wt[:], T.w[:])
 
     g_p4 = done("gq", g.iota(T.p4i[:], [[0, 32]], 0, 1))
     g_pi = done("gq", g.iota(T.pidx[:], [[0, 2]], 0, 1))
-    g_jw = done("gq", g.iota(T.jw[:], [[16, 32]], M, 0))
-    g_k16 = done("gq", g.iota(T.k16[:], [[16, 8]], 0, 0, allow_small_or_imprecise_dtypes=True))
     v_mu = done("v", V.memset(T.mu[:], 1e-35))
+    v_one = done("v", V.memset(T.ones[:], 1.0))
     need("v", g_p4)
     a = done("v", V.tensor_scalar(T.p4j[:], T.p4i[:], 3, None, A.bitwise_and))
     need("v", g_pi)
@@ -116,35 +115,37 @@ def rank_program(g, core, T, topo):
     v_qf = done("v", V.tensor_copy(T.qf[:], T.qi[:, 0:1]))
     need("v", v_hm)
     v_hn = done("v", V.tensor_scalar(T.hn[:], T.hm[:], -1.0, 1.0, A.mult, A.add))
-    need("v", v_qf, g_jw, g_k16)
-    v_j128 = done("v", V.tensor_scalar(T.j128[:], T.jw[:], T.qf[:], None, A.add))
-    a = done("v", V.tensor_scalar(T.k16q[:], T.k16[:], T.qf[:], None, A.add))
-    v_one = done("v", V.memset(T.ones[:], 1.0))
-    need("v", a)
-    v_thr = done("v", V.tensor_scalar(T.thr[:], T.k16q[:], -1.0, -0.5, A.mult, A.add))
-    v_zer = done("v", V.memset(T.zer[:], 0.0))
-    v_tb = done("v", V.memset(T.tb[:], 0.0))
-    v_rb = done("v", V.memset(T.rb[:], 0.0))
-    a = done("v", V.memset(T.evw[:, 0:M], 0.0))
-    need("v", a)
-    v_evw = done("v", V.memset(T.evw[0:32, 0:M], -1.0))
+    g_jw = done("gq", g.iota(T.jw[:], [[16, 32]], M, 0))
+    g_k16 = done("gq", g.iota(T.k16[:], [[16, 8]], 0, 0, allow_small_or_imprecise_dtypes=True))
     need("gq", v_mu)
-    g_mu = done("gq", g.affine_select(T.mu[:], T.mu[:], [[0, 4], [-1, 128]], A.is_gt, 0.0, 0, 1))
+    g_mu = done("gq", g.affine_select(T.mu[:], T.mu[:], [[-1, 128]], A.is_gt, 0.0, 0, 1))
     g_ev = done("gq", g.iota(T.evin[:], [[1, C]], 0, 0, allow_small_or_imprecise_dtypes=True))
+    need("v", v_qf, g_k16)
+    v_j = done("v", V.tensor_scalar(T.j128[:], T.jw[:], T.qf[:], None, A.add))
+    v_kq = done("v", V.tensor_scalar(T.k16q[:], T.k16[:], T.qf[:], None, A.add))
+    v_tb = [done("v", V.memset(T["tb%d" % k][:], 0.0)) for k in range(2)]
+    need("v", v_kq)
+    v_thr = done("v", V.tensor_scalar(T.thr[:], T.k16q[:], -1.0, -0.5, A.mult, A.add))
+    for k in range(2):
+        done("v", V.memset(T["rb%d" % k][:, 0:16], 0.0))
+        v_rb = done("v", V.memset(T["rb%d" % k][:, 144:160], 0.0))
 
-    need("v", ("d_sn", dma["d_sn"]), v_hn)
+    need("v", d_sn, v_hn)
     a = done("v", V.tensor_scalar(T.va[:], T.snr[:, 0:16:2], 0.0, T.hn[:], A.is_ge, A.mult))
     b = done("v", V.tensor_scalar(T.vb[:], T.snr[:, 1:16:2], 0.0, T.hm[:], A.is_ge, A.mult))
     v_sno = done("v", V.tensor_copy(T.snoff[:], T.snr[:]))
-    need("v", a, b)
+    need("v", b)
     v_vf = done("v", V.tensor_tensor(T.vf[:], T.va[:], T.vb[:], A.add))
 
-    need("s", v_off4, ("d_u", dma["d_u"]))
+    need("s", v_off4, d_u)
     s_ut = done("s", S.activation(T.ut[:], T.uw[:].indirect(T.off4[:]), F.Copy))
+    a = done("v", V.memset(T.evw[:, 0:M], 0.0))
+    need("v", a)
+    v_evw = done("v", V.memset(T.evw[0:32, 0:M], -1.0))
     need("v", s_ut)
     v_uq = done("v", V.quantize_mx(T.uq[:], T.us[:], T.ut[:]))
 
-    need("v", ("d_x", dma["d_x"]))
+    need("v", d_x)
     v_xq = done("v", V.quantize_mx(T.xq[:], T.xs[:], T.xt[:]))
     need("v", v_xq, v_sno)
     v_sl = done("v", V.tensor_copy(T.slq[:].bitcast(dt.uint32), T.xq[:].bitcast(dt.uint32).indirect(T.snoff[:, 0:16])))
@@ -169,157 +170,172 @@ def rank_program(g, core, T, topo):
             local[0] += len(es)
         g.remote_dma_fused(tr, local_sem=sem["loc"])
 
+    ec, es = _engines(T, topo, r)
     need("gq", v_vf)
-    send(_list_engines(T, topo, r), lambda d: T.vf[:, d:d + 1], T.lv[:, r:r + 1], "larr")
-    ea, eb = _data_engines(T, topo, r)
-    csrc = lambda d: T.slq[:, CAPP * d:CAPP * d + CAPP].bitcast(dt.uint8)
-    ssrc = lambda d: T.sls[:, CAPP * d:CAPP * d + CAPP]
-    cdst, sdst = T.slots[:, o:o + CAPP].bitcast(dt.uint8), T.slotss[:, o:o + CAPP]
+    send(ec, lambda d: T.vf[:, d:d + 1], T.lv[:, r:r + 1], "larr")
     need("gq", v_sl)
-    send(ea, csrc, cdst, "arrc")
-    send(eb, csrc, cdst, "arrc")
+    send(ec, lambda d: T.slq[:, CAPP * d:CAPP * d + CAPP].bitcast(dt.uint8), T.slots[:, o:o + CAPP].bitcast(dt.uint8), "arrc")
     need("gq", s_sl)
-    send(ea, ssrc, sdst, "arrs")
-    send(eb, ssrc, sdst, "arrs")
+    send(es, lambda d: T.sls[:, CAPP * d:CAPP * d + CAPP], T.slotss[:, o:o + CAPP], "arrs")
+    nc = sum(len(_engines(T, topo, s)[0][r]) for s in range(N) if s != r)
+    nl = sum(len(_engines(T, topo, s)[1][r]) for s in range(N) if s != r)
+    larr, arrc, arrs = ("larr", nc), ("arrc", nc), ("arrs", nl)
 
-    need("t", v_uq, ("d_k", dma["d_k"]))
-    t_pc = [done("t", g.tensor.matmul_mx(T["pc%d" % k][:, 0:128], T.cand[:, M + 128 * k:M + 128 * k + 128],
-                                         T.cands[:, M + 128 * k:M + 128 * k + 128], T.uq[:], T.us[:], True, True)) for k in range(4)]
-    t_row = done("t", g.tensor.matmul_mx(T.prow[:], T.uq[:], T.us[:], T.cand[:, M:M + C], T.cands[:, M:M + C], True, True))
-    t_row2 = done("t", g.tensor.matmul_mx(T.prow2[:], T.uq[:], T.us[:], T.cand[:, M:M + C], T.cands[:, M:M + C], True, True))
-    need("v", ("d_w", dma["d_w"]))
-    v_wq = done("v", V.quantize_mx(T.wq[:], T.ws[:], T.wt[:]))
-    for k in range(4):
+    need("t", v_uq)
+    t_pc, t_r, t_s = [], [], []
+    for h in range(2):
+        need("t", d_k[h])
+        for k in (2 * h, 2 * h + 1):
+            a = M + 128 * k
+            t_pc.append(done("t", g.tensor.matmul_mx(T["pc%d" % k][:, 0:128], T.cand[:, a:a + 128], T.cands[:, a:a + 128],
+                                                     T.uq[:], T.us[:], True, True)))
+        a = M + 256 * h
+        for lst, nm in ((t_r, "r"), (t_s, "s")):
+            lst.append(done("t", g.tensor.matmul_mx(T[nm + "ac"[h]][:, 0:256], T.uq[:], T.us[:], T.cand[:, a:a + 256],
+                                                    T.cands[:, a:a + 256], True, True)))
+
+    v_ns = {}
+
+    def neg(k):
         need("v", t_pc[k])
-        v_ns = done("v", V.tensor_scalar(T.ns[:, k:k + 1], T["pc%d" % k][:, 0:1], -1.0, None, A.mult))
+        v_ns[k] = done("v", V.tensor_scalar(T.ns[:, k:k + 1], T["pc%d" % k][:, 0:1], -1.0, None, A.mult))
 
-    need("s", v_ns, t_row2)
-    s_d = [done("s", S.activation(T.dd[:, 128 * k:128 * k + 128], T.prow2[:, 128 * k:128 * k + 128], F.Identity,
-                                  bias=T.ns[:, k:k + 1])) for k in range(4)]
-    need("v", t_row, v_ns)
+    def outer(k, h, lo, hi, op):
+        need("v", t_r[h], v_ns[k])
+        done("v", V.tensor_scalar(T.cm[:, 512 * k + 256 * h + lo:512 * k + 256 * h + hi], T["r" + "ac"[h]][:, lo:hi],
+                                  T.ns[:, k:k + 1], 0.0, A.add, op))
+
     v_cm = {}
-
-    def outer(k):
-        lo, hi = 128 * k, 128 * k + 128
-        if k > 0:
-            done("v", V.tensor_scalar(T.cm[:, 512 * k:512 * k + lo], T.prow[:, 0:lo], T.ns[:, k:k + 1], 0.0, A.add, A.is_le))
-        if k < 3:
-            done("v", V.tensor_scalar(T.cm[:, 512 * k + hi:512 * k + 512], T.prow[:, hi:512], T.ns[:, k:k + 1], 0.0, A.add, A.is_lt))
 
     def inner(k):
         need("v", s_d[k], g_mu)
-        v_cm[k] = done("v", V.tensor_tensor(T.cm[:, 640 * k:640 * k + 128], T.dd[:, 128 * k:128 * k + 128],
-                                            T.mu[:, 128 * k:128 * k + 128], A.is_lt))
+        v_cm[k] = done("v", V.tensor_tensor(T.cm[:, 640 * k:640 * k + 128], T.dd[:, 128 * k:128 * k + 128], T.mu[:], A.is_lt))
 
-    outer(0)
-    outer(1)
+    s_d = {}
+    neg(0)
+    neg(1)
+    outer(0, 0, 128, 256, A.is_lt)
+    outer(1, 0, 0, 128, A.is_le)
+    neg(2)
+    neg(3)
+    for h in range(2):
+        need("s", t_s[h], g_ev)
+        b = T["s" + "ac"[h]]
+        s_ev = done("s", S.activation(T.evin[32:64, 256 * h:256 * h + 256], b[32:64, 0:256], F.Copy))
+        for k in (2 * h, 2 * h + 1):
+            need("s", v_ns[k])
+            a = 128 * (k - 2 * h)
+            s_d[k] = done("s", S.activation(T.dd[:, 128 * k:128 * k + 128], b[:, a:a + 128], F.Identity, bias=T.ns[:, k:k + 1]))
+    outer(2, 0, 0, 256, A.is_le)
+    outer(0, 1, 0, 256, A.is_lt)
     inner(0)
-    outer(2)
-    inner(1)
-    outer(3)
+    outer(2, 1, 128, 256, A.is_lt)
     inner(2)
-    inner(3)
-    for k in range(3):
+    outer(1, 1, 0, 256, A.is_lt)
+    outer(3, 0, 0, 256, A.is_le)
+    outer(3, 1, 0, 128, A.is_le)
+    s_rk = {}
+
+    def total(k):
         need("s", v_cm[k])
-        s_rk = done("s", S.activation(T.junk[:, 512 * k:512 * k + 512], T.cm[:, 512 * k:512 * k + 512], F.Copy, accum_out=T.rk[:, k:k + 1]))
-    lneed = 0
-    for s in range(N):
-        if s != r:
-            lneed += len(_list_engines(T, topo, s)[r])
-    need("v", ("larr", lneed), v_one)
+        s_rk[k] = done("s", S.activation(T.junk[:, 512 * k:512 * k + 512], T.cm[:, 512 * k:512 * k + 512], F.Copy,
+                                         scale=1.0 if k < 2 else 4096.0, accum_out=T.rk[:, k:k + 1]))
+
+    g_rb = {}
+
+    def spread(k):
+        tb, tbt, rb = T["tb%d" % k], T["tbt%d" % k], T["rb%d" % k]
+        need("v", s_rk[k + 2], v_tb[k])
+        a = done("v", V.tensor_tensor(tb[:, 0:1], T.rk[:, k + 2:k + 3], T.rk[:, k:k + 1], A.add))
+        need("v", a)
+        a = done("v", V.transpose(tbt[:], tb[:]))
+        need("gq", a)
+        for q in range(4):
+            g_rb[k] = done("gq", g.partition_broadcast(rb[:, 16 + 32 * q:48 + 32 * q], tbt[32 * q:32 * q + 1, :], 128))
+
+    def unfold(k):
+        need("v", g_rb[k], v_rb)
+        n = str(k)
+        rb, t1, t2, pa, pb, pw = T["rb" + n], T["ta" + n], T["tc" + n], T["pwa" + n], T["pwb" + n], T["pw" + n]
+        a = done("v", V.transpose(t1[:], rb[:, 16:144]))
+        b = done("v", V.transpose(t2[:], rb[:]))
+        need("v", a)
+        done("v", V.tensor_scalar(pa[:, 0:8:2], t1[:, 0:128:32], T.hn[:], None, A.mult))
+        done("v", V.tensor_scalar(pb[:, 1:8:2], t1[:, 0:128:32], T.hm[:], None, A.mult))
+        need("v", b)
+        done("v", V.tensor_scalar(pb[:, 0:8:2], t2[:, 0:128:32], T.hm[:], None, A.mult))
+        a = done("v", V.tensor_scalar(pa[:, 1:8:2], t2[:, 32:160:32], T.hn[:], None, A.mult))
+        need("v", a)
+        a = done("v", V.tensor_tensor(pw[:], pa[:], pb[:], A.add))
+        need("v", a)
+        done("v", V.tensor_scalar(T.rw[:, 8 * k:8 * k + 8], pw[:], 4095, None, A.bitwise_and))
+        return done("v", V.tensor_scalar(T.rw[:, 16 + 8 * k:24 + 8 * k], pw[:], 12, None, A.arith_shift_right))
+
+    total(0)
+    total(2)
+    need("v", d_w)
+    v_wq = done("v", V.quantize_mx(T.wq[:], T.ws[:], T.wt[:]))
+    inner(1)
+    spread(0)
+    inner(3)
+    total(1)
+    total(3)
+    need("v", larr, v_one)
     for s in range(N):
         col = T.vf[:, r:r + 1] if s == r else T.lv[:, s:s + 1]
         a = done("v", V.tensor_scalar(T.bc[:, 32 * s:32 * s + 32], T.ones[:], col, None, A.mult))
     need("v", a)
     a = done("v", V.transpose(T.vrow[:], T.bc[:]))
-    need("v", a, v_zer)
-    v_pre = done("v", V.tensor_tensor_scan(T.pre[:], T.vrow[:], T.zer[:], 0.0, A.add, A.add))
-    need("v", v_cm[3])
-    v_rk = done("v", V.tensor_reduce(T.rk[:, 3:4], T.cm[:, 1536:2048], AxisListType.X, A.add))
-
-    need("v", s_rk, v_rk, v_pre)
-    a = done("v", V.tensor_scalar(T.rex[:], T.rk[:], T.pre[:, 255:256], 2048.0, A.is_ge, A.mult))
     need("v", a)
-    a = done("v", V.tensor_tensor(T.rr[:], T.rk[:], T.rex[:], A.add))
-    need("v", a)
-    a = done("v", V.tensor_scalar(T.rh[:], T.rr[:, 2:4], 4096.0, None, A.mult))
-    need("v", a, v_tb)
-    a = done("v", V.tensor_tensor(T.tb[:, 0:64:32], T.rh[:], T.rr[:, 0:2], A.add))
-    need("v", a)
-    v_tbt = done("v", V.transpose(T.tbt[:], T.tb[:]))
-    need("gq", v_tbt, v_rb)
-    for k in range(4):
-        g_rb = done("gq", g.partition_broadcast(T.rb[:, 16 + 64 * k:80 + 64 * k], T.tbt[32 * k:32 * k + 1, :], 128))
-    need("v", g_rb)
-    a = done("v", V.transpose(T.tt1[:], T.rb[:, 16:272]))
-    b = done("v", V.transpose(T.tt2[:], T.rb[:]))
-    need("v", a, b)
-    for k in range(2):
-        t1, ta, tb = T.tt1[:, 32 * k:256:64], T.tt2[:, 32 * k:256:64], T.tt2[:, 32 * k + 32:288:64]
-        done("v", V.tensor_scalar(T.pwa[:, 8 * k:8 * k + 8:2], t1, T.hn[:], None, A.mult))
-        done("v", V.tensor_scalar(T.pwb[:, 8 * k:8 * k + 8:2], ta, T.hm[:], None, A.mult))
-        done("v", V.tensor_scalar(T.pwa[:, 8 * k + 1:8 * k + 8:2], tb, T.hn[:], None, A.mult))
-        a = done("v", V.tensor_scalar(T.pwb[:, 8 * k + 1:8 * k + 8:2], t1, T.hm[:], None, A.mult))
-    need("v", a)
-    a = done("v", V.tensor_tensor(T.pw[:], T.pwa[:], T.pwb[:], A.add))
-    need("v", a)
-    done("v", V.tensor_scalar(T.rw[:, 0:16], T.pw[:], 4095, None, A.bitwise_and))
-    a = done("v", V.tensor_scalar(T.rw[:, 16:32], T.pw[:], 12, None, A.arith_shift_right))
-    need("v", a, v_j128)
-    a = done("v", V.tensor_tensor(T.fm[:], T.rw[:], T.j128[:], A.min))
-    need("v", a)
-    v_fo = done("v", V.tensor_copy(T.foff[:], T.fm[:]))
-
-    need("s", g_ev)
-    s_ev = done("s", S.activation(T.evin[32:64, :], T.prow2[32:64, :], F.Copy))
+    v_pre = done("v", V.tensor_tensor_scan(T.pre[:], T.vrow[:], T.vrow[:], 0.0, A.add, A.max))
+    spread(1)
     need("s", v_pre, v_thr)
     for k in range(8):
-        s_acc = done("s", S.activation(T.junk2[:, 256 * k:256 * k + 256], T.pre[:], F.Sign, bias=T.thr[:, k:k + 1], accum_out=T.acc[:, k:k + 1]))
-    need("v", s_acc)
-    a = done("v", V.tensor_scalar(T.sel[:], T.acc[:], -0.5, 128.0, A.mult, A.add))
+        s_acc = done("s", S.activation(T.junk2[:, 256 * k:256 * k + 255], T.pre[:, 0:255], F.Sign, bias=T.thr[:, k:k + 1], accum_out=T.acc[:, k:k + 1]))
+    unfold(0)
+    a = unfold(1)
     need("v", a)
-    v_so = done("v", V.tensor_scalar(T.soff[:], T.sel[:], 255.0, None, A.min))
+    a = done("v", V.tensor_scalar(T.ge[:], T.rw[:], T.pre[:, 255:256], 2048.0, A.is_ge, A.mult))
+    need("v", a)
+    a = done("v", V.tensor_tensor(T.rm[:], T.rw[:], T.ge[:], A.max))
+    need("v", a)
+    a = done("v", V.tensor_tensor(T.fm[:], T.rm[:], T.j128[:], A.min))
+    need("v", a)
+    v_fo = done("v", V.tensor_copy(T.foff[:], T.fm[:]))
+    need("v", s_acc)
+    v_so = done("v", V.tensor_scalar(T.soff[:], T.acc[:], -0.5, 127.5, A.mult, A.add))
 
-    need("v", s_ev, v_fo, v_evw)
-    v_ev = done("v", V.tensor_copy(T.evw[:].indirect(T.foff[:]), T.evin[:]))
-    need("y", v_ev)
-    load(Y, "d_ev", T.ev[0:1, :], T.evw[0:1, 0:M])
-    load(Y, "d_ev", T.ev[1:2, :], T.evw[32:33, 0:M])
-
-    aneed = 0
-    for s in range(N):
-        if s != r:
-            x, y = _data_engines(T, topo, s)
-            aneed += len({**x, **y}[r])
-    need("v", v_so, ("arrc", aneed), v_own)
+    need("v", v_so, arrc, v_own)
     v_ar = done("v", V.tensor_copy(T.cand[:, 0:M].bitcast(dt.uint32), T.slots[:].bitcast(dt.uint32).indirect(T.soff[:])))
-    need("s", v_so, ("arrs", aneed), s_own)
+    need("s", v_so, arrs, s_own)
     s_ar = done("s", S.activation(T.cands[:, 0:M], T.slotss[:].indirect(T.soff[:]), F.Copy))
-    need("v", v_ar, ("d_k", dma["d_k"]))
-    need("s", s_ar, v_fo, ("d_k", dma["d_k"]))
+    need("v", v_ar, v_fo, d_k[0], d_k[1])
+    need("s", s_ar, v_fo, d_k[0], d_k[1])
     v_af, s_af, t_y = [], [], []
     for k in range(2):
-        f = T.foff[:, 16 * k:16 * k + 16]
-        v_af.append(done("v", V.tensor_copy(T.aft[:, 256 * k:256 * k + 256].bitcast(dt.uint32), T.cand[:].bitcast(dt.uint32).indirect(f))))
-        s_af.append(done("s", S.activation(T.afts[:, 256 * k:256 * k + 256], T.cands[:].indirect(f), F.Copy)))
+        a, f = 256 * k, T.foff[:, 16 * k:16 * k + 16]
+        v_af.append(done("v", V.tensor_copy(T.aft[:, a:a + 256].bitcast(dt.uint32), T.cand[:].bitcast(dt.uint32).indirect(f))))
+        s_af.append(done("s", S.activation(T.afts[:, a:a + 256], T.cands[:].indirect(f), F.Copy)))
         need("t", v_af[k], s_af[k], v_wq)
-        t_y.append(done("t", g.tensor.matmul_mx(T.py[:, 512 * k:512 * k + 256], T.wq[:], T.ws[:], T.aft[:, 256 * k:256 * k + 256],
-                                                T.afts[:, 256 * k:256 * k + 256], True, True)))
+        t_y.append(done("t", g.tensor.matmul_mx(T["pc%d" % k][:, 0:256], T.wq[:], T.ws[:], T.aft[:, a:a + 256], T.afts[:, a:a + 256], True, True)))
         need("y", v_af[k])
-        load(Y, "d_out", T.oc[:, 1024 * k:1024 * k + 1024], T.aft[:, 256 * k:256 * k + 256].bitcast(dt.uint8))
-    need("s", t_y[0])
-    s_y = done("s", S.activation(T.ysb[:, 0:256], T.py[:, 0:256], F.Copy))
-    need("v", t_y[1])
-    v_y = done("v", V.tensor_copy(T.ysb[:, 256:512], T.py[:, 512:768]))
-    need("s", s_y)
-    load(S, "d_out", T.y[:, 0:256], T.ysb[:, 0:256])
+        load(Y, "d_out", T.oc[:, 4 * a:4 * a + 1024], T.aft[:, a:a + 256].bitcast(dt.uint8))
+    for k in range(2):
+        a = 256 * k
+        need("s", t_y[k])
+        s_y = done("s", S.activation(T.ysb[:, a:a + 256], T["pc%d" % k][:, 0:256], F.Copy))
+        need("s" if k else "y", s_y)
+        d_out = load(S if k else Y, "d_out", T.y[:, a:a + 256], T.ysb[:, a:a + 256])
+    need("v", s_ev, v_evw)
+    v_ev = done("v", V.tensor_copy(T.evw[:].indirect(T.foff[:]), T.evin[:]))
     need("y", s_af[1])
     for k in range(4):
-        load(Y, "d_out", T.osc[4 * k:4 * k + 4, :], T.afts[32 * k:32 * k + 4, :])
-    need("y", v_y)
-    load(Y, "d_out", T.y[:, 256:512], T.ysb[:, 256:512])
+        d_out = load(Y, "d_out", T.osc[4 * k:4 * k + 4, :], T.afts[32 * k:32 * k + 4, :])
+    need("y", v_ev)
+    load(Y, "d_ev", T.ev[0:1, :], T.evw[0:1, 0:M])
+    d_ev = load(Y, "d_ev", T.ev[1:2, :], T.evw[32:33, 0:M])
 
     for n, val in cnt.items():
         need("y", (n, val))
-    need("y", ("d_ev", dma["d_ev"]), ("d_out", dma["d_out"]))
+    need("y", d_ev, d_out)
     need("gq", ("loc", local[0]))

@@ -2,6 +2,7 @@ from concourse.bass import DstId, RemoteDMATransfer
 from concourse.mybir import dt, AluOpType as A, ActivationFunctionType as F
 
 N, CAPP, C, M = 8, 32, 512, 128
+NS = N * CAPP
 X4, U8, F32, BF, I32, U16 = "float8_e4m3fn_x4", "uint8", "float32", "bfloat16", "int32", "uint16"
 
 
@@ -12,22 +13,18 @@ def _sb(n, d):
 SCRATCH = {
     "snr": _sb(16, I32), "snoff": _sb(16, U16), "va": _sb(8, F32), "vb": _sb(8, F32), "vf": _sb(8, F32),
     "xt": _sb(1024, BF), "xq": _sb(256, X4), "xs": _sb(256, U8),
-    "slq": _sb(256, X4), "sls": _sb(256, U8), "slots": _sb(256, X4), "slotss": _sb(256, U8),
-    "cand": _sb(640, X4), "cands": _sb(640, U8), "aft": _sb(512, X4), "afts": _sb(512, U8),
+    "slq": _sb(256, X4), "sls": _sb(256, U8),
+    "cand": _sb(NS + C, X4), "cands": _sb(NS + C, U8), "aft": _sb(512, X4), "afts": _sb(512, U8),
     "uw": _sb(4, BF), "ut": _sb(512, BF), "uq": _sb(128, X4), "us": _sb(128, U8),
     "wt": _sb(512, BF), "wq": _sb(128, X4), "ws": _sb(128, U8),
     "p4i": _sb(32, I32), "p4j": _sb(32, I32), "off4": _sb(32, U16),
-    "pidx": _sb(2, I32), "hbit": _sb(2, I32), "qi": _sb(2, I32), "hm": _sb(1, F32), "hn": _sb(1, F32), "qf": _sb(1, F32),
-    "jw": _sb(32, I32), "j128": _sb(32, I32), "k16": _sb(8, F32), "k16q": _sb(8, F32), "thr": _sb(8, F32),
-    "mu": _sb(128, F32), "ones": _sb(32, F32),
-    "lv": _sb(8, F32), "bc": _sb(256, F32), "vrow": _sb(256, F32), "pre": _sb(256, F32),
-    "acc": _sb(8, F32), "soff": _sb(8, U16), "junk": _sb(2048, BF), "junk2": _sb(2048, BF),
-    "ns": _sb(4, F32), "dd": _sb(512, F32), "cm": _sb(2048, BF), "rk": _sb(4, F32),
-    "tb0": _sb(32, F32), "tb1": _sb(32, F32), "tbt0": _sb(32, F32), "tbt1": _sb(32, F32), "rb0": _sb(160, F32), "rb1": _sb(160, F32),
-    "ta0": _sb(128, F32), "ta1": _sb(128, F32), "tc0": _sb(160, F32), "tc1": _sb(160, F32),
-    "pwa0": _sb(8, F32), "pwa1": _sb(8, F32), "pwb0": _sb(8, F32), "pwb1": _sb(8, F32), "pw0": _sb(8, I32), "pw1": _sb(8, I32),
-    "rw": _sb(32, I32), "ge": _sb(32, I32), "rm": _sb(32, I32), "fm": _sb(32, I32), "foff": _sb(32, U16),
-    "evin": _sb(512, F32), "evw": _sb(640, F32), "ysb": _sb(512, F32),
+    "pidx": _sb(2, I32), "hbit": _sb(2, I32), "hm": _sb(1, F32), "hn": _sb(1, F32),
+    "mu": _sb(128, F32), "ones": _sb(32, BF), "zr": _sb(NS, BF), "j2": _sb(4, F32),
+    "lv": _sb(8, F32), "bc": _sb(256, BF), "vrow": _sb(256, BF), "pre": _sb(256, F32),
+    "sv": _sb(4, F32), "dl": _sb(4, F32), "xx": _sb(512, F32), "cm": _sb(2048, BF), "scl": _sb(1024, BF), "jk": _sb(1024, BF),
+    "ke": _sb(4, F32), "g8": _sb(8, F32), "w8": _sb(8, F32), "ab": _sb(16, F32), "zb": _sb(32, F32), "zt": _sb(32, F32),
+    "bt": _sb(64, F32), "wl": _sb(64, F32), "foff": _sb(32, U16), "eoff": _sb(16, U16),
+    "evin": _sb(256, F32), "evw": _sb(1024, F32), "evs": _sb(128, F32), "evo": _sb(128, F32), "ysb": _sb(512, F32),
     "ra": ("psum", [128, 512], F32), "rc": ("psum", [128, 512], F32), "sa": ("psum", [128, 512], F32), "sc": ("psum", [128, 512], F32),
     "pc0": ("psum", [128, 512], F32), "pc1": ("psum", [128, 512], F32), "pc2": ("psum", [128, 512], F32), "pc3": ("psum", [128, 512], F32),
 }
@@ -94,41 +91,29 @@ def rank_program(g, core, T, topo):
     d_k = []
     for k in range(2):
         a, b = 256 * k, 256 * k + 256
-        load(Y, "d_k%d" % k, T.cand[:, M + a:M + b].bitcast(dt.uint8), T.kc[:, 4 * a:4 * b])
-        d_k.append(load(Y, "d_k%d" % k, T.cands[:, M + a:M + b], T.ks[:, a:b]))
+        load(Y, "d_k%d" % k, T.cand[:, NS + a:NS + b].bitcast(dt.uint8), T.kc[:, 4 * a:4 * b])
+        d_k.append(load(Y, "d_k%d" % k, T.cands[:, NS + a:NS + b], T.ks[:, a:b]))
     d_w = load(Y, "d_w", T.wt[:], T.w[:])
 
     g_p4 = done("gq", g.iota(T.p4i[:], [[0, 32]], 0, 1))
     g_pi = done("gq", g.iota(T.pidx[:], [[0, 2]], 0, 1))
-    v_mu = done("v", V.memset(T.mu[:], 1e-35))
+    v_mu = done("v", V.memset(T.mu[:], 1.0))
     v_one = done("v", V.memset(T.ones[:], 1.0))
     need("v", g_p4)
     a = done("v", V.tensor_scalar(T.p4j[:], T.p4i[:], 3, None, A.bitwise_and))
     need("v", g_pi)
     b = done("v", V.tensor_scalar(T.hbit[:], T.pidx[:], 4, 1, A.arith_shift_right, A.bitwise_and))
-    c = done("v", V.tensor_scalar(T.qi[:], T.pidx[:], 15, None, A.bitwise_and))
     need("v", a)
     v_off4 = done("v", V.tensor_copy(T.off4[:], T.p4j[:]))
     need("v", b)
     v_hm = done("v", V.tensor_copy(T.hm[:], T.hbit[:, 0:1]))
-    need("v", c)
-    v_qf = done("v", V.tensor_copy(T.qf[:], T.qi[:, 0:1]))
     need("v", v_hm)
     v_hn = done("v", V.tensor_scalar(T.hn[:], T.hm[:], -1.0, 1.0, A.mult, A.add))
-    g_jw = done("gq", g.iota(T.jw[:], [[16, 32]], M, 0))
-    g_k16 = done("gq", g.iota(T.k16[:], [[16, 8]], 0, 0, allow_small_or_imprecise_dtypes=True))
     need("gq", v_mu)
     g_mu = done("gq", g.affine_select(T.mu[:], T.mu[:], [[-1, 128]], A.is_gt, 0.0, 0, 1))
-    g_ev = done("gq", g.iota(T.evin[:], [[1, C]], 0, 0, allow_small_or_imprecise_dtypes=True))
-    need("v", v_qf, g_k16)
-    v_j = done("v", V.tensor_scalar(T.j128[:], T.jw[:], T.qf[:], None, A.add))
-    v_kq = done("v", V.tensor_scalar(T.k16q[:], T.k16[:], T.qf[:], None, A.add))
-    v_tb = [done("v", V.memset(T["tb%d" % k][:], 0.0)) for k in range(2)]
-    need("v", v_kq)
-    v_thr = done("v", V.tensor_scalar(T.thr[:], T.k16q[:], -1.0, -0.5, A.mult, A.add))
-    for k in range(2):
-        done("v", V.memset(T["rb%d" % k][:, 0:16], 0.0))
-        v_rb = done("v", V.memset(T["rb%d" % k][:, 144:160], 0.0))
+    g_j2 = done("gq", g.iota(T.j2[:], [[256, 4]], 0, 2, allow_small_or_imprecise_dtypes=True))
+    done("v", V.memset(T.w8[:, 4:8], 0.0))
+    v_zr = done("v", V.memset(T.zr[:], 0.0))
 
     need("v", d_sn, v_hn)
     a = done("v", V.tensor_scalar(T.va[:], T.snr[:, 0:16:2], 0.0, T.hn[:], A.is_ge, A.mult))
@@ -150,11 +135,11 @@ def rank_program(g, core, T, topo):
     need("v", v_xq, v_sno)
     v_sl = done("v", V.tensor_copy(T.slq[:].bitcast(dt.uint32), T.xq[:].bitcast(dt.uint32).indirect(T.snoff[:, 0:16])))
     o = CAPP * r
-    v_own = done("v", V.tensor_copy(T.slots[:, o:o + CAPP].bitcast(dt.uint32),
+    v_own = done("v", V.tensor_copy(T.cand[:, o:o + CAPP].bitcast(dt.uint32),
                                     T.xq[:].bitcast(dt.uint32).indirect(T.snoff[:, 2 * r:2 * r + 2])))
     need("s", v_xq, v_sno)
     s_sl = done("s", S.activation(T.sls[:], T.xs[:].indirect(T.snoff[:, 0:16]), F.Copy))
-    s_own = done("s", S.activation(T.slotss[:, o:o + CAPP], T.xs[:].indirect(T.snoff[:, 2 * r:2 * r + 2]), F.Copy))
+    s_own = done("s", S.activation(T.cands[:, o:o + CAPP], T.xs[:].indirect(T.snoff[:, 2 * r:2 * r + 2]), F.Copy))
 
     local = [0]
 
@@ -174,143 +159,144 @@ def rank_program(g, core, T, topo):
     need("gq", v_vf)
     send(ec, lambda d: T.vf[:, d:d + 1], T.lv[:, r:r + 1], "larr")
     need("gq", v_sl)
-    send(ec, lambda d: T.slq[:, CAPP * d:CAPP * d + CAPP].bitcast(dt.uint8), T.slots[:, o:o + CAPP].bitcast(dt.uint8), "arrc")
+    send(ec, lambda d: T.slq[:, CAPP * d:CAPP * d + CAPP].bitcast(dt.uint8), T.cand[:, o:o + CAPP].bitcast(dt.uint8), "arrc")
     need("gq", s_sl)
-    send(es, lambda d: T.sls[:, CAPP * d:CAPP * d + CAPP], T.slotss[:, o:o + CAPP], "arrs")
+    send(es, lambda d: T.sls[:, CAPP * d:CAPP * d + CAPP], T.cands[:, o:o + CAPP], "arrs")
     nc = sum(len(_engines(T, topo, s)[0][r]) for s in range(N) if s != r)
     nl = sum(len(_engines(T, topo, s)[1][r]) for s in range(N) if s != r)
     larr, arrc, arrs = ("larr", nc), ("arrc", nc), ("arrs", nl)
+    need("gq", g_j2)
+    g_ev = done("gq", g.iota(T.evin[0:32, :], [[1, 256]], 0, 0, allow_small_or_imprecise_dtypes=True))
+    need("gq", g_ev)
+    g_ev = done("gq", g.iota(T.evin[64:96, :], [[1, 256]], 257, 0, allow_small_or_imprecise_dtypes=True))
 
     need("t", v_uq)
     t_pc, t_r, t_s = [], [], []
+
+    def row(nm, h):
+        a = NS + 256 * h
+        return done("t", g.tensor.matmul_mx(T[nm + "ac"[h]][:, 0:256], T.uq[:], T.us[:], T.cand[:, a:a + 256],
+                                            T.cands[:, a:a + 256], True, True))
+
     for h in range(2):
         need("t", d_k[h])
         for k in (2 * h, 2 * h + 1):
-            a = M + 128 * k
+            a = NS + 128 * k
             t_pc.append(done("t", g.tensor.matmul_mx(T["pc%d" % k][:, 0:128], T.cand[:, a:a + 128], T.cands[:, a:a + 128],
                                                      T.uq[:], T.us[:], True, True)))
-        a = M + 256 * h
-        for lst, nm in ((t_r, "r"), (t_s, "s")):
-            lst.append(done("t", g.tensor.matmul_mx(T[nm + "ac"[h]][:, 0:256], T.uq[:], T.us[:], T.cand[:, a:a + 256],
-                                                    T.cands[:, a:a + 256], True, True)))
-
-    v_ns = {}
-
-    def neg(k):
-        need("v", t_pc[k])
-        v_ns[k] = done("v", V.tensor_scalar(T.ns[:, k:k + 1], T["pc%d" % k][:, 0:1], -1.0, None, A.mult))
-
-    def outer(k, h, lo, hi, op):
-        need("v", t_r[h], v_ns[k])
-        done("v", V.tensor_scalar(T.cm[:, 512 * k + 256 * h + lo:512 * k + 256 * h + hi], T["r" + "ac"[h]][:, lo:hi],
-                                  T.ns[:, k:k + 1], 0.0, A.add, op))
-
-    v_cm = {}
-
-    def inner(k):
-        need("v", s_d[k], g_mu)
-        v_cm[k] = done("v", V.tensor_tensor(T.cm[:, 640 * k:640 * k + 128], T.dd[:, 128 * k:128 * k + 128], T.mu[:], A.is_lt))
-
-    s_d = {}
-    neg(0)
-    neg(1)
-    outer(0, 0, 128, 256, A.is_lt)
-    outer(1, 0, 0, 128, A.is_le)
-    neg(2)
-    neg(3)
+        t_r.append(row("r", h))
     for h in range(2):
-        need("s", t_s[h], g_ev)
-        b = T["s" + "ac"[h]]
-        s_ev = done("s", S.activation(T.evin[32:64, 256 * h:256 * h + 256], b[32:64, 0:256], F.Copy))
+        t_s.append(row("s", h))
+
+    v_sv = {}
+    for k in range(2):
+        need("v", t_pc[k])
+        v_sv[k] = done("v", V.tensor_copy(T.sv[:, k:k + 1], T["pc%d" % k][:, 0:1]))
+    s_x = {}
+
+    def thresholds(h):
+        need("s", v_sv[2 * h], v_sv[2 * h + 1], g_mu)
+        a = done("s", S.activation(T.dl[:, 2 * h:2 * h + 2], T.sv[:, 2 * h:2 * h + 2], F.Abs, scale=0.74 * 2.0 ** -23, bias=2e-38))
+        need("s", a)
         for k in (2 * h, 2 * h + 1):
-            need("s", v_ns[k])
-            a = 128 * (k - 2 * h)
-            s_d[k] = done("s", S.activation(T.dd[:, 128 * k:128 * k + 128], b[:, a:a + 128], F.Identity, bias=T.ns[:, k:k + 1]))
-    outer(2, 0, 0, 256, A.is_le)
-    outer(0, 1, 0, 256, A.is_lt)
-    inner(0)
-    outer(2, 1, 128, 256, A.is_lt)
-    inner(2)
-    outer(1, 1, 0, 256, A.is_lt)
-    outer(3, 0, 0, 256, A.is_le)
-    outer(3, 1, 0, 128, A.is_le)
-    s_rk = {}
+            s_x[k] = done("s", S.activation(T.xx[:, 128 * k:128 * k + 128], T.mu[:], F.Identity, bias=T.sv[:, k:k + 1], scale=T.dl[:, k:k + 1]))
 
-    def total(k):
-        need("s", v_cm[k])
-        s_rk[k] = done("s", S.activation(T.junk[:, 512 * k:512 * k + 512], T.cm[:, 512 * k:512 * k + 512], F.Copy,
-                                         scale=1.0 if k < 2 else 4096.0, accum_out=T.rk[:, k:k + 1]))
-
-    g_rb = {}
-
-    def spread(k):
-        tb, tbt, rb = T["tb%d" % k], T["tbt%d" % k], T["rb%d" % k]
-        need("v", s_rk[k + 2], v_tb[k])
-        a = done("v", V.tensor_tensor(tb[:, 0:1], T.rk[:, k + 2:k + 3], T.rk[:, k:k + 1], A.add))
-        need("v", a)
-        a = done("v", V.transpose(tbt[:], tb[:]))
-        need("gq", a)
-        for q in range(4):
-            g_rb[k] = done("gq", g.partition_broadcast(rb[:, 16 + 32 * q:48 + 32 * q], tbt[32 * q:32 * q + 1, :], 128))
-
-    def unfold(k):
-        need("v", g_rb[k], v_rb)
-        n = str(k)
-        rb, t1, t2, pa, pb, pw = T["rb" + n], T["ta" + n], T["tc" + n], T["pwa" + n], T["pwb" + n], T["pw" + n]
-        a = done("v", V.transpose(t1[:], rb[:, 16:144]))
-        b = done("v", V.transpose(t2[:], rb[:]))
-        need("v", a)
-        done("v", V.tensor_scalar(pa[:, 0:8:2], t1[:, 0:128:32], T.hn[:], None, A.mult))
-        done("v", V.tensor_scalar(pb[:, 1:8:2], t1[:, 0:128:32], T.hm[:], None, A.mult))
-        need("v", b)
-        done("v", V.tensor_scalar(pb[:, 0:8:2], t2[:, 0:128:32], T.hm[:], None, A.mult))
-        a = done("v", V.tensor_scalar(pa[:, 1:8:2], t2[:, 32:160:32], T.hn[:], None, A.mult))
-        need("v", a)
-        a = done("v", V.tensor_tensor(pw[:], pa[:], pb[:], A.add))
-        need("v", a)
-        done("v", V.tensor_scalar(T.rw[:, 8 * k:8 * k + 8], pw[:], 4095, None, A.bitwise_and))
-        return done("v", V.tensor_scalar(T.rw[:, 16 + 8 * k:24 + 8 * k], pw[:], 12, None, A.arith_shift_right))
-
-    total(0)
-    total(2)
-    need("v", d_w)
-    v_wq = done("v", V.quantize_mx(T.wq[:], T.ws[:], T.wt[:]))
-    inner(1)
-    spread(0)
-    inner(3)
-    total(1)
-    total(3)
-    need("v", larr, v_one)
+    thresholds(0)
+    for k in range(2, 4):
+        need("s", t_pc[k])
+        v_sv[k] = done("s", S.activation(T.sv[:, k:k + 1], T["pc%d" % k][:, 0:1], F.Copy))
+    thresholds(1)
+    need("s", larr, v_one, v_vf)
     for s in range(N):
         col = T.vf[:, r:r + 1] if s == r else T.lv[:, s:s + 1]
-        a = done("v", V.tensor_scalar(T.bc[:, 32 * s:32 * s + 32], T.ones[:], col, None, A.mult))
-    need("v", a)
-    a = done("v", V.transpose(T.vrow[:], T.bc[:]))
-    need("v", a)
-    v_pre = done("v", V.tensor_tensor_scan(T.pre[:], T.vrow[:], T.vrow[:], 0.0, A.add, A.max))
-    spread(1)
-    need("s", v_pre, v_thr)
-    for k in range(8):
-        s_acc = done("s", S.activation(T.junk2[:, 256 * k:256 * k + 255], T.pre[:, 0:255], F.Sign, bias=T.thr[:, k:k + 1], accum_out=T.acc[:, k:k + 1]))
-    unfold(0)
-    a = unfold(1)
-    need("v", a)
-    a = done("v", V.tensor_scalar(T.ge[:], T.rw[:], T.pre[:, 255:256], 2048.0, A.is_ge, A.mult))
-    need("v", a)
-    a = done("v", V.tensor_tensor(T.rm[:], T.rw[:], T.ge[:], A.max))
-    need("v", a)
-    a = done("v", V.tensor_tensor(T.fm[:], T.rm[:], T.j128[:], A.min))
-    need("v", a)
-    v_fo = done("v", V.tensor_copy(T.foff[:], T.fm[:]))
-    need("v", s_acc)
-    v_so = done("v", V.tensor_scalar(T.soff[:], T.acc[:], -0.5, 127.5, A.mult, A.add))
+        s_bc = done("s", S.activation(T.bc[:, CAPP * s:CAPP * s + CAPP], T.ones[:], F.Copy, scale=col))
+    for h in range(2):
+        need("s", t_s[h])
+        s_ev = done("s", S.activation(T.evin[32 + 64 * h:64 + 64 * h, :], T["s" + "ac"[h]][32 + 64 * h:64 + 64 * h, 0:256], F.Copy))
 
-    need("v", v_so, arrc, v_own)
-    v_ar = done("v", V.tensor_copy(T.cand[:, 0:M].bitcast(dt.uint32), T.slots[:].bitcast(dt.uint32).indirect(T.soff[:])))
-    need("s", v_so, arrs, s_own)
-    s_ar = done("s", S.activation(T.cands[:, 0:M], T.slotss[:].indirect(T.soff[:]), F.Copy))
-    need("v", v_ar, v_fo, d_k[0], d_k[1])
-    need("s", s_ar, v_fo, d_k[0], d_k[1])
+    v_cm, v_sc = {}, {}
+
+    def outer(k, h, lo, hi, op):
+        need("v", t_r[h], v_sv[k])
+        v_cm[k] = done("v", V.tensor_scalar(T.cm[:, 512 * k + 256 * h + lo:512 * k + 256 * h + hi], T["r" + "ac"[h]][:, lo:hi],
+                                            T.sv[:, k:k + 1], None, op))
+
+    def inner(k):
+        a = 128 * (k % 2)
+        need("v", s_x[k], t_r[k // 2])
+        v_cm[k] = done("v", V.tensor_tensor(T.cm[:, 640 * k:640 * k + 128], T["r" + "ac"[k // 2]][:, a:a + 128],
+                                            T.xx[:, 128 * k:128 * k + 128], A.is_lt))
+
+    def total(k):
+        need("v", v_cm[k])
+        v_sc[k] = done("v", V.tensor_tensor_scan(T.scl[:, 256 * k:256 * k + 256], T.cm[:, 512 * k:512 * k + 256],
+                                                 T.cm[:, 512 * k + 256:512 * k + 512], -256.0, A.add, A.add))
+
+    def stay(k):
+        need("v", v_sc[k], v_pre, g_j2)
+        return done("v", V.tensor_scalar(T.w8[:, k:k + 1], T.scl[:, 256 * k + 255:256 * k + 256], T.pre[:, 255:256],
+                                         T.j2[:, k:k + 1], A.is_ge, A.mult))
+
+    outer(1, 0, 0, 128, A.is_le)
+    outer(0, 0, 128, 256, A.is_lt)
+    inner(0)
+    inner(1)
+    outer(2, 0, 0, 256, A.is_le)
+    outer(3, 0, 0, 256, A.is_le)
+    outer(0, 1, 0, 256, A.is_lt)
+    outer(1, 1, 0, 256, A.is_lt)
+    total(0)
+    need("v", s_bc)
+    v_vr = done("v", V.transpose(T.vrow[:], T.bc[:]))
+    total(1)
+    need("v", v_vr, v_zr)
+    v_pre = done("v", V.tensor_tensor_scan(T.pre[:], T.vrow[:], T.zr[:], -256.5, A.add, A.add))
+    outer(2, 1, 128, 256, A.is_lt)
+    inner(2)
+    stay(0)
+    outer(3, 1, 0, 128, A.is_le)
+    total(2)
+    inner(3)
+    stay(1)
+    total(3)
+    stay(2)
+    for k in range(4):
+        need("s", v_pre, v_sc[k])
+        s_acc = done("s", S.activation(T.jk[:, 256 * k:256 * k + 256], T.pre[:], F.Sign, bias=T.scl[:, 256 * k + 255:256 * k + 256],
+                                       scale=-1.0, accum_out=T.g8[:, k:k + 1]))
+    v_w8 = stay(3)
+    v_ke = done("v", V.tensor_scalar(T.ke[:], T.scl[:, 255:1024:256], T.pre[:, 255:256], 512.0, A.is_ge, A.mult))
+    need("v", d_w)
+    v_wq = done("v", V.quantize_mx(T.wq[:], T.ws[:], T.wt[:]))
+    need("v", v_ke)
+    v_e = done("v", V.tensor_tensor(T.g8[:, 4:8], T.ke[:], T.scl[:, 255:1024:256], A.add))
+
+    need("v", s_acc, v_w8, v_e)
+    for c in range(2):
+        for h in range(2):
+            v_ab = done("v", V.tensor_tensor(T.ab[64 * h:64 * h + 64, c:16:2], T.g8[64 * c:64 * c + 64, :], T.w8[64 * c:64 * c + 64, :], A.add))
+    need("v", v_ab)
+    need("s", v_ab)
+    for q in range(2):
+        for c in range(2):
+            a, b = 32 * q, 32 * c
+            v_zb = done("v", V.tensor_copy(T.zb[a:a + 32, c:32:2], T.ab[b:b + 32, :]))
+            s_zb = done("s", S.activation(T.zb[64 + a:96 + a, c:32:2], T.ab[64 + b:96 + b, :], F.Copy))
+    need("v", v_zb, s_zb)
+    v_zt = done("v", V.transpose(T.zt[:], T.zb[:]))
+    need("v", v_zt)
+    need("s", v_zt)
+    for h in range(2):
+        v_bt = done("v", V.tensor_copy(T.bt[:, 16 * h:16 * h + 16], T.zt[:, 0:16]))
+        s_bt = done("s", S.activation(T.bt[:, 32 + 16 * h:48 + 16 * h], T.zt[:, 16:32], F.Copy))
+    need("v", v_bt, s_bt)
+    v_wl = done("v", V.transpose(T.wl[:], T.bt[:]))
+    need("v", v_wl)
+    for b in range(2):
+        v_fo = done("v", V.tensor_scalar(T.foff[:, b:32:2], T.wl[:, 32 * b:32 * b + 16], 0.5, 128.0, A.mult, A.add))
+
+    need("v", v_fo, arrc, v_own, d_k[0], d_k[1])
+    need("s", v_fo, arrs, s_own, d_k[0], d_k[1])
     v_af, s_af, t_y = [], [], []
     for k in range(2):
         a, f = 256 * k, T.foff[:, 16 * k:16 * k + 16]
@@ -325,15 +311,24 @@ def rank_program(g, core, T, topo):
         need("s", t_y[k])
         s_y = done("s", S.activation(T.ysb[:, a:a + 256], T["pc%d" % k][:, 0:256], F.Copy))
         need("s" if k else "y", s_y)
-        d_out = load(S if k else Y, "d_out", T.y[:, a:a + 256], T.ysb[:, a:a + 256])
-    need("v", s_ev, v_evw)
-    v_ev = done("v", V.tensor_copy(T.evw[:].indirect(T.foff[:]), T.evin[:]))
+        load(S if k else Y, "d_out", T.y[:, a:a + 256], T.ysb[:, a:a + 256])
+    for h in range(2):
+        for b in range(2):
+            c = 32 * b + 16 + 8 * h
+            v_eo = done("v", V.tensor_scalar(T.eoff[64 * h:64 * h + 64, b:16:2], T.wl[64 * h:64 * h + 64, c:c + 8], 256.0, None, A.add))
+    need("v", v_eo, s_ev, g_ev, v_evw)
+    a = done("v", V.tensor_copy(T.evw[:].indirect(T.eoff[:]), T.evin[:]))
+    need("v", a)
+    a = done("v", V.tensor_copy(T.evs[0:64, :], T.evw[64:128, 0:M]))
+    need("v", a)
+    v_ev = done("v", V.tensor_tensor(T.evo[0:64, :], T.evw[0:64, 0:M], T.evs[0:64, :], A.add))
     need("y", s_af[1])
     for k in range(4):
         d_out = load(Y, "d_out", T.osc[4 * k:4 * k + 4, :], T.afts[32 * k:32 * k + 4, :])
     need("y", v_ev)
-    load(Y, "d_ev", T.ev[0:1, :], T.evw[0:1, 0:M])
-    d_ev = load(Y, "d_ev", T.ev[1:2, :], T.evw[32:33, 0:M])
+    need("s", v_ev)
+    load(Y, "d_ev", T.ev[0:1, :], T.evo[0:1, :])
+    d_ev = load(S, "d_ev", T.ev[1:2, :], T.evo[32:33, :])
 
     for n, val in cnt.items():
         need("y", (n, val))

from concourse.bass import DstId, RemoteDMATransfer
from concourse.mybir import dt, AluOpType as A, ActivationFunctionType as F

N, CAPP, C, M = 8, 32, 512, 128
NS = N * CAPP
X4, U8, F32, BF, I32, U16 = "float8_e4m3fn_x4", "uint8", "float32", "bfloat16", "int32", "uint16"


def _sb(n, d):
    return ("sbuf", [128, n], d)


SCRATCH = {
    "snr": _sb(16, I32), "snoff": _sb(16, U16), "va": _sb(8, F32), "vb": _sb(8, F32), "vf": _sb(8, F32),
    "xt": _sb(1024, BF), "xq": _sb(256, X4), "xs": _sb(256, U8),
    "slq": _sb(256, X4), "sls": _sb(256, U8),
    "cand": _sb(NS + C, X4), "cands": _sb(NS + C, U8), "aft": _sb(512, X4), "afts": _sb(512, U8),
    "uw": _sb(4, BF), "ut": _sb(512, BF), "uq": _sb(128, X4), "us": _sb(128, U8),
    "wt": _sb(512, BF), "wq": _sb(128, X4), "ws": _sb(128, U8),
    "p4i": _sb(32, I32), "p4j": _sb(32, I32), "off4": _sb(32, U16),
    "pidx": _sb(2, I32), "hbit": _sb(2, I32), "hm": _sb(1, F32), "hn": _sb(1, F32),
    "mu": _sb(128, F32), "ones": _sb(32, BF), "zr": _sb(NS, BF), "j2": _sb(4, F32),
    "lv": _sb(8, F32), "bc": _sb(256, BF), "vrow": _sb(256, BF), "pre": _sb(256, F32),
    "sv": _sb(4, F32), "dl": _sb(4, F32), "xx": _sb(512, F32), "cm": _sb(2048, BF), "scl": _sb(1024, BF), "jk": _sb(1024, BF),
    "ke": _sb(4, F32), "g8": _sb(8, F32), "w8": _sb(8, F32), "ab": _sb(16, F32), "zb": _sb(32, F32), "zt": _sb(32, F32),
    "bt": _sb(64, F32), "wl": _sb(64, F32), "foff": _sb(32, U16), "eoff": _sb(16, U16),
    "evin": _sb(256, F32), "evw": _sb(1024, F32), "evs": _sb(128, F32), "evo": _sb(128, F32), "ysb": _sb(512, F32),
    "ra": ("psum", [128, 512], F32), "rc": ("psum", [128, 512], F32), "sa": ("psum", [128, 512], F32), "sc": ("psum", [128, 512], F32),
    "pc0": ("psum", [128, 512], F32), "pc1": ("psum", [128, 512], F32), "pc2": ("psum", [128, 512], F32), "pc3": ("psum", [128, 512], F32),
}
SEMAPHORES = ["v", "s", "t", "gq", "d_sn", "d_x", "d_u", "d_k0", "d_k1", "d_w", "d_ev", "d_out", "larr", "arrc", "arrs", "loc"]


def _deal(dst, engs):
    r, k = {}, 0
    two = len(engs) - len(dst)
    for n, d in enumerate(dst):
        w = 2 if n >= len(dst) - two else 1
        r[d] = engs[k:k + w]
        k += w
    return r


def _engines(T, topo, s):
    me = T.cores[s]
    rest = [(s + k) % N for k in range(1, N)]
    on = [d for d in rest if topo.chip(T.cores[d]) == topo.chip(me)]
    off = [d for d in rest if topo.chip(T.cores[d]) != topo.chip(me)]
    e_off = topo.engines(me, T.cores[off[0]])
    e_on = [e for e in topo.engines(me, T.cores[on[0]]) if e not in e_off]
    h = len(e_off) // 2
    a = _deal(off, e_off)
    b = _deal(off[2:] + off[:2], e_off[h:] + e_off[:h])
    a[on[0]] = b[on[0]] = e_on[:len(e_on) // 4]
    return a, b


def rank_program(g, core, T, topo):
    r = T.rank_of(core)
    if r is None:
        return
    sem = T.sem
    cnt = {"v": 0, "s": 0, "t": 0, "gq": 0}
    seen = {}
    qs = {"v": g.vector, "s": g.scalar, "t": g.tensor, "gq": g, "y": g.sync}

    def need(q, *deps):
        for name, val in deps:
            if seen.get((q, name), 0) < val:
                qs[q].wait_ge(sem[name], val)
                seen[(q, name)] = val

    def done(q, ins):
        ins.then_inc(sem[q], 1)
        cnt[q] += 1
        return (q, cnt[q])

    V, S, Y = g.vector, g.scalar, g.sync
    dma = {}

    def load(q, name, out, in_):
        q.dma_start(out, in_).then_inc(sem[name], 16)
        dma[name] = dma.get(name, 0) + 16
        return (name, dma[name])

    for k in range(4):
        load(Y, "d_sn", T.snr[16 * k:16 * k + 16, :], T.sn[:])
        d_sn = load(S, "d_sn", T.snr[64 + 16 * k:80 + 16 * k, :], T.sn[:])
    d_u = load(S, "d_u", T.uw[:], T.u[:, 0:4])
    d_x = load(Y, "d_x", T.xt[:], T.x[:])
    d_k = []
    for k in range(2):
        a, b = 256 * k, 256 * k + 256
        load(Y, "d_k%d" % k, T.cand[:, NS + a:NS + b].bitcast(dt.uint8), T.kc[:, 4 * a:4 * b])
        d_k.append(load(Y, "d_k%d" % k, T.cands[:, NS + a:NS + b], T.ks[:, a:b]))
    d_w = load(Y, "d_w", T.wt[:], T.w[:])

    g_p4 = done("gq", g.iota(T.p4i[:], [[0, 32]], 0, 1))
    g_pi = done("gq", g.iota(T.pidx[:], [[0, 2]], 0, 1))
    v_mu = done("v", V.memset(T.mu[:], 1.0))
    v_one = done("v", V.memset(T.ones[:], 1.0))
    need("v", g_p4)
    a = done("v", V.tensor_scalar(T.p4j[:], T.p4i[:], 3, None, A.bitwise_and))
    need("v", g_pi)
    b = done("v", V.tensor_scalar(T.hbit[:], T.pidx[:], 4, 1, A.arith_shift_right, A.bitwise_and))
    need("v", a)
    v_off4 = done("v", V.tensor_copy(T.off4[:], T.p4j[:]))
    need("v", b)
    v_hm = done("v", V.tensor_copy(T.hm[:], T.hbit[:, 0:1]))
    need("v", v_hm)
    v_hn = done("v", V.tensor_scalar(T.hn[:], T.hm[:], -1.0, 1.0, A.mult, A.add))
    need("gq", v_mu)
    g_mu = done("gq", g.affine_select(T.mu[:], T.mu[:], [[-1, 128]], A.is_gt, 0.0, 0, 1))
    g_j2 = done("gq", g.iota(T.j2[:], [[256, 4]], 0, 2, allow_small_or_imprecise_dtypes=True))
    done("v", V.memset(T.w8[:, 4:8], 0.0))
    v_zr = done("v", V.memset(T.zr[:], 0.0))

    need("v", d_sn, v_hn)
    a = done("v", V.tensor_scalar(T.va[:], T.snr[:, 0:16:2], 0.0, T.hn[:], A.is_ge, A.mult))
    b = done("v", V.tensor_scalar(T.vb[:], T.snr[:, 1:16:2], 0.0, T.hm[:], A.is_ge, A.mult))
    v_sno = done("v", V.tensor_copy(T.snoff[:], T.snr[:]))
    need("v", b)
    v_vf = done("v", V.tensor_tensor(T.vf[:], T.va[:], T.vb[:], A.add))

    need("s", v_off4, d_u)
    s_ut = done("s", S.activation(T.ut[:], T.uw[:].indirect(T.off4[:]), F.Copy))
    a = done("v", V.memset(T.evw[:, 0:M], 0.0))
    need("v", a)
    v_evw = done("v", V.memset(T.evw[0:32, 0:M], -1.0))
    need("v", s_ut)
    v_uq = done("v", V.quantize_mx(T.uq[:], T.us[:], T.ut[:]))

    need("v", d_x)
    v_xq = done("v", V.quantize_mx(T.xq[:], T.xs[:], T.xt[:]))
    need("v", v_xq, v_sno)
    v_sl = done("v", V.tensor_copy(T.slq[:].bitcast(dt.uint32), T.xq[:].bitcast(dt.uint32).indirect(T.snoff[:, 0:16])))
    o = CAPP * r
    v_own = done("v", V.tensor_copy(T.cand[:, o:o + CAPP].bitcast(dt.uint32),
                                    T.xq[:].bitcast(dt.uint32).indirect(T.snoff[:, 2 * r:2 * r + 2])))
    need("s", v_xq, v_sno)
    s_sl = done("s", S.activation(T.sls[:], T.xs[:].indirect(T.snoff[:, 0:16]), F.Copy))
    s_own = done("s", S.activation(T.cands[:, o:o + CAPP], T.xs[:].indirect(T.snoff[:, 2 * r:2 * r + 2]), F.Copy))

    local = [0]

    def send(engs, src, dst, rs):
        tr = []
        for d, es in engs.items():
            rid, pid, _ = topo.addr(T.cores[d])
            m = 0
            for e in es:
                m |= 1 << e
            tr.append(RemoteDMATransfer(dst_ids=[DstId(rid=rid, pnc=pid)], dma_engine_mask=m, remote_sem=sem[rs],
                                        srcs=[src(d)], dsts=[dst]))
            local[0] += len(es)
        g.remote_dma_fused(tr, local_sem=sem["loc"])

    ec, es = _engines(T, topo, r)
    need("gq", v_vf)
    send(ec, lambda d: T.vf[:, d:d + 1], T.lv[:, r:r + 1], "larr")
    need("gq", v_sl)
    send(ec, lambda d: T.slq[:, CAPP * d:CAPP * d + CAPP].bitcast(dt.uint8), T.cand[:, o:o + CAPP].bitcast(dt.uint8), "arrc")
    need("gq", s_sl)
    send(es, lambda d: T.sls[:, CAPP * d:CAPP * d + CAPP], T.cands[:, o:o + CAPP], "arrs")
    nc = sum(len(_engines(T, topo, s)[0][r]) for s in range(N) if s != r)
    nl = sum(len(_engines(T, topo, s)[1][r]) for s in range(N) if s != r)
    larr, arrc, arrs = ("larr", nc), ("arrc", nc), ("arrs", nl)
    need("gq", g_j2)
    g_ev = done("gq", g.iota(T.evin[0:32, :], [[1, 256]], 0, 0, allow_small_or_imprecise_dtypes=True))
    need("gq", g_ev)
    g_ev = done("gq", g.iota(T.evin[64:96, :], [[1, 256]], 257, 0, allow_small_or_imprecise_dtypes=True))

    need("t", v_uq)
    t_pc, t_r, t_s = [], [], []

    def row(nm, h):
        a = NS + 256 * h
        return done("t", g.tensor.matmul_mx(T[nm + "ac"[h]][:, 0:256], T.uq[:], T.us[:], T.cand[:, a:a + 256],
                                            T.cands[:, a:a + 256], True, True))

    for h in range(2):
        need("t", d_k[h])
        for k in (2 * h, 2 * h + 1):
            a = NS + 128 * k
            t_pc.append(done("t", g.tensor.matmul_mx(T["pc%d" % k][:, 0:128], T.cand[:, a:a + 128], T.cands[:, a:a + 128],
                                                     T.uq[:], T.us[:], True, True)))
        t_r.append(row("r", h))
    for h in range(2):
        t_s.append(row("s", h))

    v_sv = {}
    for k in range(2):
        need("v", t_pc[k])
        v_sv[k] = done("v", V.tensor_copy(T.sv[:, k:k + 1], T["pc%d" % k][:, 0:1]))
    s_x = {}

    def thresholds(h):
        need("s", v_sv[2 * h], v_sv[2 * h + 1], g_mu)
        a = done("s", S.activation(T.dl[:, 2 * h:2 * h + 2], T.sv[:, 2 * h:2 * h + 2], F.Abs, scale=0.74 * 2.0 ** -23, bias=2e-38))
        need("s", a)
        for k in (2 * h, 2 * h + 1):
            s_x[k] = done("s", S.activation(T.xx[:, 128 * k:128 * k + 128], T.mu[:], F.Identity, bias=T.sv[:, k:k + 1], scale=T.dl[:, k:k + 1]))

    thresholds(0)
    for k in range(2, 4):
        need("s", t_pc[k])
        v_sv[k] = done("s", S.activation(T.sv[:, k:k + 1], T["pc%d" % k][:, 0:1], F.Copy))
    thresholds(1)
    need("s", larr, v_one, v_vf)
    for s in range(N):
        col = T.vf[:, r:r + 1] if s == r else T.lv[:, s:s + 1]
        s_bc = done("s", S.activation(T.bc[:, CAPP * s:CAPP * s + CAPP], T.ones[:], F.Copy, scale=col))
    for h in range(2):
        need("s", t_s[h])
        s_ev = done("s", S.activation(T.evin[32 + 64 * h:64 + 64 * h, :], T["s" + "ac"[h]][32 + 64 * h:64 + 64 * h, 0:256], F.Copy))

    v_cm, v_sc = {}, {}

    def outer(k, h, lo, hi, op):
        need("v", t_r[h], v_sv[k])
        v_cm[k] = done("v", V.tensor_scalar(T.cm[:, 512 * k + 256 * h + lo:512 * k + 256 * h + hi], T["r" + "ac"[h]][:, lo:hi],
                                            T.sv[:, k:k + 1], None, op))

    def inner(k):
        a = 128 * (k % 2)
        need("v", s_x[k], t_r[k // 2])
        v_cm[k] = done("v", V.tensor_tensor(T.cm[:, 640 * k:640 * k + 128], T["r" + "ac"[k // 2]][:, a:a + 128],
                                            T.xx[:, 128 * k:128 * k + 128], A.is_lt))

    def total(k):
        need("v", v_cm[k])
        v_sc[k] = done("v", V.tensor_tensor_scan(T.scl[:, 256 * k:256 * k + 256], T.cm[:, 512 * k:512 * k + 256],
                                                 T.cm[:, 512 * k + 256:512 * k + 512], -256.0, A.add, A.add))

    def stay(k):
        need("v", v_sc[k], v_pre, g_j2)
        return done("v", V.tensor_scalar(T.w8[:, k:k + 1], T.scl[:, 256 * k + 255:256 * k + 256], T.pre[:, 255:256],
                                         T.j2[:, k:k + 1], A.is_ge, A.mult))

    outer(1, 0, 0, 128, A.is_le)
    outer(0, 0, 128, 256, A.is_lt)
    inner(0)
    inner(1)
    outer(2, 0, 0, 256, A.is_le)
    outer(3, 0, 0, 256, A.is_le)
    outer(0, 1, 0, 256, A.is_lt)
    outer(1, 1, 0, 256, A.is_lt)
    total(0)
    need("v", s_bc)
    v_vr = done("v", V.transpose(T.vrow[:], T.bc[:]))
    total(1)
    need("v", v_vr, v_zr)
    v_pre = done("v", V.tensor_tensor_scan(T.pre[:], T.vrow[:], T.zr[:], -256.5, A.add, A.add))
    outer(2, 1, 128, 256, A.is_lt)
    inner(2)
    stay(0)
    outer(3, 1, 0, 128, A.is_le)
    total(2)
    inner(3)
    stay(1)
    total(3)
    stay(2)
    for k in range(4):
        need("s", v_pre, v_sc[k])
        s_acc = done("s", S.activation(T.jk[:, 256 * k:256 * k + 256], T.pre[:], F.Sign, bias=T.scl[:, 256 * k + 255:256 * k + 256],
                                       scale=-1.0, accum_out=T.g8[:, k:k + 1]))
    v_w8 = stay(3)
    v_ke = done("v", V.tensor_scalar(T.ke[:], T.scl[:, 255:1024:256], T.pre[:, 255:256], 512.0, A.is_ge, A.mult))
    need("v", d_w)
    v_wq = done("v", V.quantize_mx(T.wq[:], T.ws[:], T.wt[:]))
    need("v", v_ke)
    v_e = done("v", V.tensor_tensor(T.g8[:, 4:8], T.ke[:], T.scl[:, 255:1024:256], A.add))

    need("v", s_acc, v_w8, v_e)
    for c in range(2):
        for h in range(2):
            v_ab = done("v", V.tensor_tensor(T.ab[64 * h:64 * h + 64, c:16:2], T.g8[64 * c:64 * c + 64, :], T.w8[64 * c:64 * c + 64, :], A.add))
    need("v", v_ab)
    need("s", v_ab)
    for q in range(2):
        for c in range(2):
            a, b = 32 * q, 32 * c
            v_zb = done("v", V.tensor_copy(T.zb[a:a + 32, c:32:2], T.ab[b:b + 32, :]))
            s_zb = done("s", S.activation(T.zb[64 + a:96 + a, c:32:2], T.ab[64 + b:96 + b, :], F.Copy))
    need("v", v_zb, s_zb)
    v_zt = done("v", V.transpose(T.zt[:], T.zb[:]))
    need("v", v_zt)
    need("s", v_zt)
    for h in range(2):
        v_bt = done("v", V.tensor_copy(T.bt[:, 16 * h:16 * h + 16], T.zt[:, 0:16]))
        s_bt = done("s", S.activation(T.bt[:, 32 + 16 * h:48 + 16 * h], T.zt[:, 16:32], F.Copy))
    need("v", v_bt, s_bt)
    v_wl = done("v", V.transpose(T.wl[:], T.bt[:]))
    need("v", v_wl)
    for b in range(2):
        v_fo = done("v", V.tensor_scalar(T.foff[:, b:32:2], T.wl[:, 32 * b:32 * b + 16], 0.5, 128.0, A.mult, A.add))

    need("v", v_fo, arrc, v_own, d_k[0], d_k[1])
    need("s", v_fo, arrs, s_own, d_k[0], d_k[1])
    v_af, s_af, t_y = [], [], []
    for k in range(2):
        a, f = 256 * k, T.foff[:, 16 * k:16 * k + 16]
        v_af.append(done("v", V.tensor_copy(T.aft[:, a:a + 256].bitcast(dt.uint32), T.cand[:].bitcast(dt.uint32).indirect(f))))
        s_af.append(done("s", S.activation(T.afts[:, a:a + 256], T.cands[:].indirect(f), F.Copy)))
        need("t", v_af[k], s_af[k], v_wq)
        t_y.append(done("t", g.tensor.matmul_mx(T["pc%d" % k][:, 0:256], T.wq[:], T.ws[:], T.aft[:, a:a + 256], T.afts[:, a:a + 256], True, True)))
        need("y", v_af[k])
        load(Y, "d_out", T.oc[:, 4 * a:4 * a + 1024], T.aft[:, a:a + 256].bitcast(dt.uint8))
    for k in range(2):
        a = 256 * k
        need("s", t_y[k])
        s_y = done("s", S.activation(T.ysb[:, a:a + 256], T["pc%d" % k][:, 0:256], F.Copy))
        need("s" if k else "y", s_y)
        load(S if k else Y, "d_out", T.y[:, a:a + 256], T.ysb[:, a:a + 256])
    for h in range(2):
        for b in range(2):
            c = 32 * b + 16 + 8 * h
            v_eo = done("v", V.tensor_scalar(T.eoff[64 * h:64 * h + 64, b:16:2], T.wl[64 * h:64 * h + 64, c:c + 8], 256.0, None, A.add))
    need("v", v_eo, s_ev, g_ev, v_evw)
    a = done("v", V.tensor_copy(T.evw[:].indirect(T.eoff[:]), T.evin[:]))
    need("v", a)
    a = done("v", V.tensor_copy(T.evs[0:64, :], T.evw[64:128, 0:M]))
    need("v", a)
    v_ev = done("v", V.tensor_tensor(T.evo[0:64, :], T.evw[0:64, 0:M], T.evs[0:64, :], A.add))
    need("y", s_af[1])
    for k in range(4):
        d_out = load(Y, "d_out", T.osc[4 * k:4 * k + 4, :], T.afts[32 * k:32 * k + 4, :])
    need("y", v_ev)
    need("s", v_ev)
    load(Y, "d_ev", T.ev[0:1, :], T.evo[0:1, :])
    d_ev = load(S, "d_ev", T.ev[1:2, :], T.evo[32:33, :])

    for n, val in cnt.items():
        need("y", (n, val))
    need("y", d_ev, d_out)
    need("gq", ("loc", local[0]))
